import numpy as np
import ml_dtypes


def mxq(x, axis, fmt="e4m3"):
    dtype, down = {"e4m3": (ml_dtypes.float8_e4m3fn, 7), "e5m2": (ml_dtypes.float8_e5m2, 14)}[fmt]
    v = np.moveaxis(np.asarray(x, np.float32).astype(ml_dtypes.bfloat16).astype(np.float64), axis, -1)
    blocks = v.reshape(v.shape[:-1] + (-1, 32))
    amax = np.abs(blocks).max(-1, keepdims=True)
    byte = np.maximum(np.where(amax > 0, np.frexp(amax)[1] - 1 + 127, 0) - down, 1)
    scale = np.exp2(byte - 127.0)
    codes = (blocks / scale).astype(np.float32).astype(dtype).astype(np.float64)
    return np.moveaxis((codes * scale).reshape(v.shape), -1, axis)


WIDE = False


def mx_kscale(k):
    if not WIDE:
        return np.ones(k)
    levels = np.array([10, -10, 5, -5, 0])
    if k % 512:
        return np.exp2(np.random.permutation(np.resize(levels, k // 32))).repeat(32)
    a = np.empty((k // 512, 16))
    for p in range(k // 512):
        a[p, :8] = np.random.permutation(np.resize(levels, 8))
        for g in range(8):
            far = levels[np.abs(levels - a[p, g]) >= 10]
            a[p, g + 8] = far[np.random.randint(len(far))]
    return np.exp2(a.ravel()).repeat(32)


def f64(x):
    return np.asarray(x).astype(np.float64)


def striped(idx):
    return np.tile(np.asarray(idx).reshape(-1, 16).T, (8, 1)).astype(np.uint16)


def unstriped(offs):
    return offs[:16].T.reshape(-1).astype(np.int64)


E2M1 = np.array([0.0, 0.5, 1.0, 1.5, 2.0, 3.0, 4.0, 6.0, -0.0, -0.5, -1.0, -1.5, -2.0, -3.0, -4.0, -6.0])


def pack_weight(w, fmt):
    k, n = w.shape
    w = f64(np.asarray(w, np.float32).astype(ml_dtypes.bfloat16)).reshape(k // 32, 32, n)
    amax = np.abs(w).max(1)
    if fmt == "e4m3":
        byte = np.frexp(amax)[1] - 1 + 127 - 7
    else:
        mant, ex = np.frexp(amax / 6.0)
        byte = np.where(mant > 0.5, ex, ex - 1) + 127
    byte = np.clip(np.where(amax > 0, byte, 1), 1, 254)
    scaled = (w * np.exp2(127.0 - byte)[:, None, :]).reshape(k, n).astype(np.float32)
    by_word = np.ascontiguousarray(scaled.reshape(k // 512, 128, 4, n).transpose(0, 1, 3, 2))
    if fmt == "e4m3":
        words = by_word.astype(ml_dtypes.float8_e4m3fn).view(np.uint8)
    else:
        c = by_word.astype(ml_dtypes.float4_e2m1fn).view(np.uint8) & 0xF
        words = (c[..., 0::2] | (c[..., 1::2] << 4)).reshape(k // 512, 128, 2 * n)
    return np.ascontiguousarray(words), np.ascontiguousarray(byte.astype(np.uint8).reshape(k // 512, 16, n))


def unpack_weight(words, scales, fmt):
    g, _, n = scales.shape
    words = np.ascontiguousarray(words).reshape(g, 128, n, -1)
    if fmt == "e4m3":
        vals = words.view(ml_dtypes.float8_e4m3fn).astype(np.float64)
    else:
        nib = np.empty((g, 128, n, 4), np.uint8)
        nib[..., 0::2] = words & 0xF
        nib[..., 1::2] = words >> 4
        vals = E2M1[nib]
    vals = vals * np.repeat(np.exp2(scales.astype(np.float64) - 127.0), 8, axis=1)[..., None]
    return vals.transpose(0, 1, 3, 2).reshape(g * 512, n)


def sigmoid(v):
    return 1.0 / (1.0 + np.exp(-v))


def bf(x):
    return np.asarray(x, np.float32).astype(ml_dtypes.bfloat16)


def planes(Y):
    r, m = Y.shape
    b = f64(bf(Y)).reshape(r // 32, 32, m)
    amax = np.abs(b).max(1)
    byte = np.clip(np.where(amax > 0, np.frexp(amax)[1] - 1 + 127 - 7, 1), 1, 254)
    codes = (b * np.exp2(127.0 - byte)[:, None, :]).reshape(r, m).astype(np.float32).astype(ml_dtypes.float8_e4m3fn).view(np.uint8)
    words = codes.reshape(r // 512, 128, 4, m).transpose(0, 1, 3, 2)
    return np.ascontiguousarray(words), np.ascontiguousarray(byte.astype(np.uint8).reshape(r // 512, 16, m))


D, T, I, Q, E = 512, 2048, 512, 256, 512


def setup_inputs():
    n = np.random.standard_normal
    idx = np.random.permutation(T)[:I]
    fd = mx_kscale(D)
    fi = mx_kscale(I)
    ti = np.ones(T)
    ti[idx] = fi
    keysp = pack_weight(n((D, T)) / fd[:, None], "e2m1")
    return {
        "query": (n((D, Q)) * 0.4 / np.sqrt(D) * fd[:, None]).astype(np.float32),
        "keys_words": keysp[0],
        "keys_scales": keysp[1],
        "size": (np.random.uniform(8.0, 24.0, (1, I)) * fi).astype(np.float32),
        "vals": (n((E, T)) / ti).astype(np.float32),
        "gval": (n((E, T)) / ti).astype(np.float32),
        "offs": striped(idx),
    }


def reference(query, keys_words, keys_scales, size, vals, gval, offs):
    idx = unstriped(offs)
    keysu = unpack_weight(keys_words, keys_scales, "e2m1")
    queryq = mxq(f64(query), 0, "e4m3")
    keysidxg = keysu[:, idx]
    a = queryq.T @ keysidxg
    p = np.exp(a - np.max(a, axis=1, keepdims=True))
    w = p * f64(size) / np.sum(p, axis=1, keepdims=True)
    wt = w.T
    vt = f64(vals)[:, idx].T
    ut = f64(gval)[:, idx].T
    vtq = mxq(vt, 0, "e4m3")
    wtq = mxq(wt, 0, "e4m3")
    o = vtq.T @ wtq
    utq = mxq(ut, 0, "e4m3")
    u = utq.T @ wtq
    y = o * sigmoid(u)
    words, scales = planes(y)
    return y, words, scales

@@ -1,0 +1,195 @@
+from contextlib import ExitStack
+
+import concourse.mybir as mybir
+from concourse.masks import make_identity
+
+D, T, I, Q, E = 512, 2048, 512, 256, 512
+FLOPS = 2 * Q * I * (D + 2 * E)
+
+F32 = mybir.dt.float32
+BF16 = mybir.dt.bfloat16
+I32 = mybir.dt.int32
+U32 = mybir.dt.uint32
+U16 = mybir.dt.uint16
+U8 = mybir.dt.uint8
+FP8X4 = mybir.dt.float8_e4m3fn_x4
+FP4X4 = mybir.dt.float4_e2m1fn_x4
+ACT = mybir.ActivationFunctionType
+ALU = mybir.AluOpType
+AXIS = mybir.AxisListType
+
+P = 128
+PACK = 4
+HALVES = Q // P
+SLABS = 2 * PACK
+SLAB_BYTES = 4 * T
+
+
+def tile_attend_gatedvalues_pl_kernel(tc, query, keys_words, keys_scales, size, vals, gval, offs, out_0, out_1, out_2):
+    nc = tc.nc
+    with ExitStack() as ctx:
+        keep = ctx.enter_context(tc.tile_pool(name="keep", bufs=1))
+        ring = ctx.enter_context(tc.tile_pool(name="ring", bufs=2))
+        slabs = ctx.enter_context(tc.tile_pool(name="slabs", bufs=1))
+        psum = ctx.enter_context(tc.psum_pool(name="psum", bufs=2))
+
+        offsets = keep.tile([P, I // 16], U16, name="offsets")
+        nc.sync.dma_start(offsets[:], offs)
+
+        key_pool = keep.tile([P, T], U16, name="key_pool", align_bytes=64)
+        nc.sync.dma_start(key_pool[:].bitcast(I32), keys_words[0].bitcast(I32))
+        key_scale_pool = keep.tile([P, T], U8, name="key_scale_pool", align_bytes=64)
+        nc.gpsimd.memset(key_scale_pool[:].bitcast(I32), 0)
+        for quad in range(4):
+            nc.sync.dma_start(
+                key_scale_pool[32 * quad : 32 * quad + 4, :].bitcast(I32),
+                keys_scales[0, 4 * quad : 4 * quad + 4, :].bitcast(I32),
+            )
+        slot_size = keep.tile([P, PACK], F32, name="slot_size")
+        nc.scalar.dma_start(slot_size[:], size.rearrange("o (s r) -> (o s) r", r=PACK))
+
+        warm_in = keep.tile([P, 1], F32, name="warm_in")
+        warm_out = keep.tile([P, 1], F32, name="warm_out")
+        nc.vector.memset(warm_in[:], 0.0)
+        nc.scalar.activation(warm_out[:], warm_in[:], ACT.Exp)
+
+        q_raw = keep.tile([P, PACK, Q], F32, name="q_raw")
+        nc.sync.dma_start(q_raw[:], query.rearrange("(p j) q -> p j q", j=PACK))
+
+        gate_rows = gval.rearrange("(p t) c -> t p c", t=PACK)
+        value_rows = vals.rearrange("(p t) c -> t p c", t=PACK)
+        pools = []
+        for n in range(SLABS):
+            pools.append(slabs.tile([P, T], F32, name="pool%d" % n, offset=n * SLAB_BYTES))
+            nc.sync.dma_start(pools[n][:], (gate_rows, value_rows)[n % 2][n // 2])
+
+        ident = keep.tile([P, P], F32, name="ident")
+        make_identity(nc, ident[:])
+
+        key_words = keep.tile([P, I], U16, name="key_words", align_bytes=64)
+        key_scales = keep.tile([P, I], U8, name="key_scales", align_bytes=64)
+        nc.vector.tensor_copy(key_words[:], key_pool[:].indirect(offsets[:]))
+        nc.vector.tensor_copy(key_scales[:], key_scale_pool[:].indirect(offsets[:]))
+
+        q_bf = keep.tile([P, Q, PACK], BF16, name="q_bf", align_bytes=64)
+        nc.scalar.copy(
+            q_bf[:].rearrange("p (c i) j -> p c j i", i=4),
+            q_raw[:].rearrange("p j (c i) -> p c j i", i=4),
+        )
+        q_codes = keep.tile([P, Q], U32, name="q_codes", align_bytes=64)
+        q_scales = keep.tile([P, Q], U8, name="q_scales", align_bytes=64)
+        nc.vector.quantize_mx(q_codes[:].bitcast(FP8X4), q_scales[:], q_bf[:].rearrange("p q j -> p (q j)"))
+
+        def pick_and_turn(n):
+            picked = ring.tile([P, I], BF16, name="picked", align_bytes=64)
+            nc.vector.tensor_copy(picked[:], pools[n][:].indirect(offsets[:]))
+            pairs = picked[:].bitcast(F32)
+            turned = psum.tile([P, 2, P], F32, name="turned")
+            for u in range(2):
+                nc.tensor.transpose(turned[:, u, :], pairs[:, u::2], ident[:])
+            grouped = ring.tile([P, P * PACK], BF16, name="grouped", align_bytes=64, bufs=3)
+            nc.scalar.copy(
+                grouped[:].bitcast(F32).rearrange("p (e u) -> p e u", u=2),
+                turned[:].rearrange("p u e -> p e u"),
+            )
+            return grouped
+
+        def quantise(n, grouped):
+            if n + 1 < SLABS:
+                codes = slabs.tile([P, P], U32, name="codes%d" % n, offset=(n + 1) * SLAB_BYTES, align_bytes=64)
+            else:
+                codes = keep.tile([P, P], U32, name="codes%d" % n, align_bytes=64)
+            scales = keep.tile([P, P], U8, name="scales%d" % n, align_bytes=64)
+            nc.vector.quantize_mx(codes[:].bitcast(FP8X4), scales[:], grouped[:])
+            return codes, scales
+
+        w_bf = keep.tile([P, Q, PACK], BF16, name="w_bf", align_bytes=64)
+        scores, neg_max, prob, row_sum = [], [], [], []
+        for h in range(HALVES):
+            cols = slice(h * P, (h + 1) * P)
+            scores.append(psum.tile([P, I], F32, name="softmax_bank"))
+            nc.tensor.matmul_mx(
+                scores[h][:],
+                lhsT=q_codes[:, cols].bitcast(FP8X4), lhsT_scale=q_scales[:, cols],
+                rhs=key_words[:].bitcast(FP4X4), rhs_scale=key_scales[:],
+                start=True, stop=True,
+            )
+        for h in range(HALVES):
+            neg_max.append(keep.tile([P, 1], F32, name="neg_max%d" % h))
+            nc.vector.tensor_reduce(neg_max[h][:], scores[h][:], AXIS.X, ALU.max, negate=True)
+            prob.append(keep.tile([P, PACK, P], F32, name="prob%d" % h))
+            row_sum.append(keep.tile([P, 1], F32, name="row_sum%d" % h))
+            nc.scalar.activation(
+                prob[h][:], scores[h][:].rearrange("p (s r) -> p r s", r=PACK), ACT.Exp,
+                bias=neg_max[h][:], accum_out=row_sum[h][:],
+            )
+        grouped = [pick_and_turn(0)]
+        for h in range(HALVES):
+            inv_sum = keep.tile([P, 1], F32, name="inv_sum%d" % h)
+            nc.vector.reciprocal(inv_sum[:], row_sum[h][:])
+            normed = keep.tile([P, PACK, P], F32, name="normed%d" % h)
+            nc.scalar.activation(normed[:], prob[h][:], ACT.Copy, scale=inv_sum[:])
+            by_slot = psum.tile([P, PACK, P], F32, name="softmax_bank")
+            for r in range(PACK):
+                nc.tensor.transpose(by_slot[:, r, :], normed[:, r, :], ident[:])
+            nc.vector.tensor_tensor(
+                w_bf[:, h * P : (h + 1) * P, :],
+                by_slot[:].rearrange("p r q -> p q r"),
+                slot_size[:].unsqueeze(1).to_broadcast([P, P, PACK]),
+                ALU.mult,
+            )
+        w_codes = keep.tile([P, Q], U32, name="w_codes", align_bytes=64)
+        w_scales = keep.tile([P, Q], U8, name="w_scales", align_bytes=64)
+        nc.vector.quantize_mx(w_codes[:].bitcast(FP8X4), w_scales[:], w_bf[:].rearrange("p q j -> p (q j)"))
+
+        def weighted_sum(operand, name):
+            codes, scales = operand
+            acc = psum.tile([P, Q], F32, name=name)
+            nc.tensor.matmul_mx(
+                acc[:],
+                lhsT=codes[:].bitcast(FP8X4), lhsT_scale=scales[:],
+                rhs=w_codes[:].bitcast(FP8X4), rhs_scale=w_scales[:],
+                start=True, stop=True,
+            )
+            return acc
+
+        y_rows = out_0.rearrange("(p t) q -> p t q", t=PACK)
+        y_bf = keep.tile([P, Q, PACK], BF16, name="y_bf", align_bytes=64)
+        y_last = keep.tile([P, 2, Q], F32, name="y_last")
+        gates, value_sums = {}, {}
+
+        def gated(t):
+            if t < 2:
+                y = slabs.tile([P, Q], F32, name="y%d" % t, offset=(2 * t + 3) * SLAB_BYTES + 1024)
+                y = y[:]
+            else:
+                y = y_last[:, t - 2, :]
+            nc.vector.tensor_tensor(y, value_sums[t][:], gates[t][:], ALU.mult)
+            (nc.sync if t < 3 else nc.scalar).dma_start(y_rows[:, t, :], y)
+            if t < 2:
+                nc.scalar.copy(y_bf[:, :, t], y)
+
+        for n in range(SLABS):
+            if n + 1 < SLABS:
+                grouped.append(pick_and_turn(n + 1))
+            operand = quantise(n, grouped[n])
+            if n % 2 == 0:
+                gates[n // 2] = keep.tile([P, Q], F32, name="gate%d" % (n // 2))
+                nc.scalar.activation(gates[n // 2][:], weighted_sum(operand, "gate_sum")[:], ACT.Sigmoid)
+                if n > 0:
+                    gated(n // 2 - 1)
+            else:
+                value_sums[n // 2] = weighted_sum(operand, "value_sum")
+        gated(PACK - 1)
+        nc.vector.tensor_copy(y_bf[:, :, 2:4], y_last[:].rearrange("p t q -> p q t"))
+
+        y_codes = keep.tile([P, Q], U32, name="y_codes", align_bytes=64)
+        y_scales = keep.tile([P, Q], U8, name="y_scales", align_bytes=64)
+        nc.vector.quantize_mx(y_codes[:].bitcast(FP8X4), y_scales[:], y_bf[:].rearrange("p q j -> p (q j)"))
+        nc.sync.dma_start(out_1[0].rearrange("p q j -> p (q j)").bitcast(I32), y_codes[:].bitcast(I32))
+        for quad in range(4):
+            queue = nc.scalar if quad % 2 == 0 else nc.sync
+            queue.dma_start(
+                out_2[0, 4 * quad : 4 * quad + 4, :].bitcast(I32),
+                y_scales[32 * quad : 32 * quad + 4, :].bitcast(I32),
+            )

@@ -33,11 +33,10 @@ def tile_attend_gatedvalues_pl_kernel(tc, query, keys_words, keys_scales, size, 
         slabs = ctx.enter_context(tc.tile_pool(name="slabs", bufs=1))
         psum = ctx.enter_context(tc.psum_pool(name="psum", bufs=2))
 
-        offsets = keep.tile([P, I // 16], U16, name="offsets")
-        nc.sync.dma_start(offsets[:], offs)
-
         key_pool = keep.tile([P, T], U16, name="key_pool", align_bytes=64)
         nc.sync.dma_start(key_pool[:].bitcast(I32), keys_words[0].bitcast(I32))
+        offsets = keep.tile([P, I // 16], U16, name="offsets")
+        nc.sync.dma_start(offsets[:], offs)
         key_scale_pool = keep.tile([P, T], U8, name="key_scale_pool", align_bytes=64)
         nc.gpsimd.memset(key_scale_pool[:].bitcast(I32), 0)
         for quad in range(4):
@@ -58,10 +57,11 @@ def tile_attend_gatedvalues_pl_kernel(tc, query, keys_words, keys_scales, size, 
 
         gate_rows = gval.rearrange("(p t) c -> t p c", t=PACK)
         value_rows = vals.rearrange("(p t) c -> t p c", t=PACK)
+        slab_rows = [gate_rows[t] for t in range(PACK)] + [value_rows[t] for t in range(PACK)]
         pools = []
         for n in range(SLABS):
             pools.append(slabs.tile([P, T], F32, name="pool%d" % n, offset=n * SLAB_BYTES))
-            nc.sync.dma_start(pools[n][:], (gate_rows, value_rows)[n % 2][n // 2])
+            nc.sync.dma_start(pools[n][:], slab_rows[n])
 
         ident = keep.tile([P, P], F32, name="ident")
         make_identity(nc, ident[:])
@@ -80,31 +80,29 @@ def tile_attend_gatedvalues_pl_kernel(tc, query, keys_words, keys_scales, size, 
         q_scales = keep.tile([P, Q], U8, name="q_scales", align_bytes=64)
         nc.vector.quantize_mx(q_codes[:].bitcast(FP8X4), q_scales[:], q_bf[:].rearrange("p q j -> p (q j)"))
 
-        def pick_and_turn(n):
+        def pick_and_turn(n, turned):
             picked = ring.tile([P, I], BF16, name="picked", align_bytes=64)
             nc.vector.tensor_copy(picked[:], pools[n][:].indirect(offsets[:]))
             pairs = picked[:].bitcast(F32)
-            turned = psum.tile([P, 2, P], F32, name="turned")
             for u in range(2):
                 nc.tensor.transpose(turned[:, u, :], pairs[:, u::2], ident[:])
-            grouped = ring.tile([P, P * PACK], BF16, name="grouped", align_bytes=64, bufs=3)
+
+        def regroup(turned, grouped):
             nc.scalar.copy(
-                grouped[:].bitcast(F32).rearrange("p (e u) -> p e u", u=2),
-                turned[:].rearrange("p u e -> p e u"),
+                grouped.bitcast(F32).rearrange("p (n e u) -> p n e u", e=P, u=2),
+                turned.rearrange("p n u e -> p n e u"),
             )
-            return grouped
 
-        def quantise(n, grouped):
-            if n + 1 < SLABS:
-                codes = slabs.tile([P, P], U32, name="codes%d" % n, offset=(n + 1) * SLAB_BYTES, align_bytes=64)
-            else:
-                codes = keep.tile([P, P], U32, name="codes%d" % n, align_bytes=64)
-            scales = keep.tile([P, P], U8, name="scales%d" % n, align_bytes=64)
-            nc.vector.quantize_mx(codes[:].bitcast(FP8X4), scales[:], grouped[:])
-            return codes, scales
+        def quantise(grouped, codes):
+            scales = keep.tile([P, codes.shape[1]], U8, name="scales%d" % len(planes), align_bytes=64)
+            planes.append(scales)
+            nc.vector.quantize_mx(codes.bitcast(FP8X4), scales[:], grouped)
+            return codes, scales[:]
 
-        w_bf = keep.tile([P, Q, PACK], BF16, name="w_bf", align_bytes=64)
-        scores, neg_max, prob, row_sum = [], [], [], []
+        planes = []
+        scores, neg_max, prob = [], [], []
+        row_sum = keep.tile([P, HALVES], F32, name="row_sum")
+        inv_sum = keep.tile([P, HALVES], F32, name="inv_sum")
         for h in range(HALVES):
             cols = slice(h * P, (h + 1) * P)
             scores.append(psum.tile([P, I], F32, name="softmax_bank"))
@@ -118,74 +116,110 @@ def tile_attend_gatedvalues_pl_kernel(tc, query, keys_words, keys_scales, size, 
             neg_max.append(keep.tile([P, 1], F32, name="neg_max%d" % h))
             nc.vector.tensor_reduce(neg_max[h][:], scores[h][:], AXIS.X, ALU.max, negate=True)
             prob.append(keep.tile([P, PACK, P], F32, name="prob%d" % h))
-            row_sum.append(keep.tile([P, 1], F32, name="row_sum%d" % h))
             nc.scalar.activation(
                 prob[h][:], scores[h][:].rearrange("p (s r) -> p r s", r=PACK), ACT.Exp,
-                bias=neg_max[h][:], accum_out=row_sum[h][:],
+                bias=neg_max[h][:], accum_out=row_sum[:, h : h + 1],
             )
-        grouped = [pick_and_turn(0)]
+        turned = psum.tile([P, 2, 2, P], F32, name="turned")
+        pick_and_turn(0, turned[:, 0])
+        pick_and_turn(1, turned[:, 1])
+        nc.vector.reciprocal(inv_sum[:], row_sum[:])
+        by_slot = []
         for h in range(HALVES):
-            inv_sum = keep.tile([P, 1], F32, name="inv_sum%d" % h)
-            nc.vector.reciprocal(inv_sum[:], row_sum[h][:])
             normed = keep.tile([P, PACK, P], F32, name="normed%d" % h)
-            nc.scalar.activation(normed[:], prob[h][:], ACT.Copy, scale=inv_sum[:])
-            by_slot = psum.tile([P, PACK, P], F32, name="softmax_bank")
+            nc.scalar.activation(normed[:], prob[h][:], ACT.Copy, scale=inv_sum[:, h : h + 1])
+            by_slot.append(psum.tile([P, PACK, P], F32, name="softmax_bank"))
             for r in range(PACK):
-                nc.tensor.transpose(by_slot[:, r, :], normed[:, r, :], ident[:])
-            nc.vector.tensor_tensor(
-                w_bf[:, h * P : (h + 1) * P, :],
-                by_slot[:].rearrange("p r q -> p q r"),
-                slot_size[:].unsqueeze(1).to_broadcast([P, P, PACK]),
-                ALU.mult,
-            )
-        w_codes = keep.tile([P, Q], U32, name="w_codes", align_bytes=64)
-        w_scales = keep.tile([P, Q], U8, name="w_scales", align_bytes=64)
-        nc.vector.quantize_mx(w_codes[:].bitcast(FP8X4), w_scales[:], w_bf[:].rearrange("p q j -> p (q j)"))
+                nc.tensor.transpose(by_slot[h][:, r, :], normed[:, r, :], ident[:])
 
-        def weighted_sum(operand, name):
+        def weighted_sum(acc, operand, n, rows=slice(0, Q)):
             codes, scales = operand
-            acc = psum.tile([P, Q], F32, name=name)
+            cols = slice(n * P, (n + 1) * P)
             nc.tensor.matmul_mx(
-                acc[:],
-                lhsT=codes[:].bitcast(FP8X4), lhsT_scale=scales[:],
-                rhs=w_codes[:].bitcast(FP8X4), rhs_scale=w_scales[:],
+                acc,
+                lhsT=codes[:, cols].bitcast(FP8X4), lhsT_scale=scales[:, cols],
+                rhs=w_codes[:, rows].bitcast(FP8X4), rhs_scale=w_scales[:, rows],
                 start=True, stop=True,
             )
-            return acc
+
+        def pair_sums(operand, name):
+            sums = psum.tile([P, 2, Q], F32, name=name)
+            for n in range(2):
+                weighted_sum(sums[:, n, :], operand, n)
+            return sums
+
+        def sigmoid(gate, gate_sum):
+            half_tanh = ring.tile([P, 2, Q], F32, name="half_tanh")
+            nc.scalar.activation(half_tanh[:], gate_sum, ACT.Tanh, scale=0.5)
+            nc.scalar.activation(gate, half_tanh[:], ACT.Copy, scale=0.5, bias=0.5)
 
         y_rows = out_0.rearrange("(p t) q -> p t q", t=PACK)
+        gates = keep.tile([P, PACK, Q], F32, name="gates")
+        w_scales = keep.tile([P, Q], U8, name="w_scales", align_bytes=64)
+
+        operands = []
+        for k in range(3):
+            grouped = ring.tile([P, 2 * I], BF16, name="grouped", align_bytes=64)
+            regroup(turned[:], grouped[:])
+            turned = psum.tile([P, 2, 2, P], F32, name="turned")
+            pick_and_turn(2 * k + 2, turned[:, 0])
+            reuse = (2 * k + 2) * SLAB_BYTES
+            codes = slabs.tile([P, 2 * P], U32, name="codes%d" % k, offset=reuse, align_bytes=64)
+            operands.append(quantise(grouped[:], codes[:]))
+            if k == 0:
+                w_bf = slabs.tile([P, Q, PACK], BF16, name="w_bf", offset=reuse + 2048, align_bytes=64)
+                for h in range(HALVES):
+                    nc.vector.tensor_tensor(
+                        w_bf[:, h * P : (h + 1) * P, :],
+                        by_slot[h][:].rearrange("p r q -> p q r"),
+                        slot_size[:].unsqueeze(1).to_broadcast([P, P, PACK]),
+                        ALU.mult,
+                    )
+            if k < 2:
+                pick_and_turn(2 * k + 3, turned[:, 1])
+            if k == 0:
+                w_codes = slabs.tile([P, Q], U32, name="w_codes", offset=reuse + SLAB_BYTES, align_bytes=64)
+                nc.vector.quantize_mx(w_codes[:].bitcast(FP8X4), w_scales[:], w_bf[:].rearrange("p q j -> p (q j)"))
+            if k < 2:
+                sigmoid(gates[:, 2 * k : 2 * k + 2, :], pair_sums(operands[k], "gate_sum")[:])
+        first_sums = pair_sums(operands[2], "value_sum")
+
+        grouped = ring.tile([P, I], BF16, name="grouped", align_bytes=64)
+        regroup(turned[:, 0:1], grouped[:])
+        turned = psum.tile([P, 1, 2, P], F32, name="turned")
+        pick_and_turn(7, turned[:, 0])
+        codes = slabs.tile([P, P], U32, name="codes6", offset=7 * SLAB_BYTES, align_bytes=64)
+        value_sum = psum.tile([P, Q], F32, name="value_sum")
+        weighted_sum(value_sum[:], quantise(grouped[:], codes[:]), 0)
+        y_first = slabs.tile([P, 2, Q], F32, name="y_first", offset=7 * SLAB_BYTES + 2048)
+        nc.vector.tensor_tensor(y_first[:], first_sums[:], gates[:, 0:2, :], ALU.mult)
+        nc.sync.dma_start(y_rows[:, 0:2, :], y_first[:])
+        grouped = slabs.tile([P, I], BF16, name="grouped7", offset=SLABS * SLAB_BYTES, align_bytes=64)
+        regroup(turned[:], grouped[:])
         y_bf = keep.tile([P, Q, PACK], BF16, name="y_bf", align_bytes=64)
-        y_last = keep.tile([P, 2, Q], F32, name="y_last")
-        gates, value_sums = {}, {}
-
-        def gated(t):
-            if t < 2:
-                y = slabs.tile([P, Q], F32, name="y%d" % t, offset=(2 * t + 3) * SLAB_BYTES + 1024)
-                y = y[:]
-            else:
-                y = y_last[:, t - 2, :]
-            nc.vector.tensor_tensor(y, value_sums[t][:], gates[t][:], ALU.mult)
-            (nc.sync if t < 3 else nc.scalar).dma_start(y_rows[:, t, :], y)
-            if t < 2:
-                nc.scalar.copy(y_bf[:, :, t], y)
-
-        for n in range(SLABS):
-            if n + 1 < SLABS:
-                grouped.append(pick_and_turn(n + 1))
-            operand = quantise(n, grouped[n])
-            if n % 2 == 0:
-                gates[n // 2] = keep.tile([P, Q], F32, name="gate%d" % (n // 2))
-                nc.scalar.activation(gates[n // 2][:], weighted_sum(operand, "gate_sum")[:], ACT.Sigmoid)
-                if n > 0:
-                    gated(n // 2 - 1)
-            else:
-                value_sums[n // 2] = weighted_sum(operand, "value_sum")
-        gated(PACK - 1)
-        nc.vector.tensor_copy(y_bf[:, :, 2:4], y_last[:].rearrange("p t q -> p q t"))
+        nc.scalar.copy(y_bf[:, :, 0:2], y_first[:].rearrange("p t q -> p q t"))
+        codes = keep.tile([P, P], U32, name="codes7", align_bytes=64)
+        operand = quantise(grouped[:], codes[:])
+        halves = [slice(h * P, (h + 1) * P) for h in range(HALVES)]
+        last_sums = [psum.tile([P, P], F32, name=name) for name in ("gate_sum", "gate_sum")]
+        for h in range(HALVES):
+            weighted_sum(last_sums[h][:], operand, 0, halves[h])
+        y_last = slabs.tile([P, 2, Q], F32, name="y_last", offset=SLABS * SLAB_BYTES)
+        nc.vector.tensor_tensor(y_last[:, 0, :], value_sum[:], gates[:, 2, :], ALU.mult)
+        nc.sync.dma_start(y_rows[:, 2, :], y_last[:, 0, :])
+        for h in range(HALVES):
+            nc.vector.tensor_tensor(y_last[:, 1, halves[h]], last_sums[h][:], gates[:, 3, halves[h]], ALU.mult)
+        nc.scalar.dma_start(y_rows[:, 3, :], y_last[:, 1, :])
+        for h in range(HALVES):
+            nc.vector.tensor_copy(y_bf[:, halves[h], 2:4], y_last[:, :, halves[h]].rearrange("p t q -> p q t"))
 
         y_codes = keep.tile([P, Q], U32, name="y_codes", align_bytes=64)
         y_scales = keep.tile([P, Q], U8, name="y_scales", align_bytes=64)
-        nc.vector.quantize_mx(y_codes[:].bitcast(FP8X4), y_scales[:], y_bf[:].rearrange("p q j -> p (q j)"))
+        for h in range(HALVES):
+            nc.vector.quantize_mx(
+                y_codes[:, halves[h]].bitcast(FP8X4), y_scales[:, halves[h]],
+                y_bf[:, halves[h], :].rearrange("p q j -> p (q j)"),
+            )
         nc.sync.dma_start(out_1[0].rearrange("p q j -> p (q j)").bitcast(I32), y_codes[:].bitcast(I32))
         for quad in range(4):
             queue = nc.scalar if quad % 2 == 0 else nc.sync

@@ -168,13 +168,19 @@ def tile_attend_gatedvalues_pl_kernel(tc, query, keys_words, keys_scales, size, 
             operands.append(quantise(grouped[:], codes[:]))
             if k == 0:
                 w_bf = slabs.tile([P, Q, PACK], BF16, name="w_bf", offset=reuse + 2048, align_bytes=64)
-                for h in range(HALVES):
-                    nc.vector.tensor_tensor(
-                        w_bf[:, h * P : (h + 1) * P, :],
-                        by_slot[h][:].rearrange("p r q -> p q r"),
-                        slot_size[:].unsqueeze(1).to_broadcast([P, P, PACK]),
-                        ALU.mult,
-                    )
+                nc.vector.tensor_tensor(
+                    w_bf[:, 0:P, :],
+                    by_slot[0][:].rearrange("p r q -> p q r"),
+                    slot_size[:].unsqueeze(1).to_broadcast([P, P, PACK]),
+                    ALU.mult,
+                )
+                w_rows = keep.tile([P, PACK, P], BF16, name="w_rows")
+                for r in range(PACK):
+                    nc.scalar.activation(w_rows[:, r, :], by_slot[1][:, r, :], ACT.Copy, scale=slot_size[:, r : r + 1])
+                nc.scalar.copy(
+                    w_bf[:, P:Q, :].rearrange("p (c i) r -> p c r i", i=4),
+                    w_rows[:].rearrange("p r (c i) -> p c r i", i=4),
+                )
             if k < 2:
                 pick_and_turn(2 * k + 3, turned[:, 1])
             if k == 0:

@@ -21,8 +21,15 @@ AXIS = mybir.AxisListType
 P = 128
 PACK = 4
 HALVES = Q // P
-SLABS = 2 * PACK
 SLAB_BYTES = 4 * T
+
+
+def dealt(row):
+    return row.rearrange("p (u g c) -> p g u c", u=2, c=16)
+
+
+def listed(row):
+    return row.rearrange("p (g u c) -> p g u c", u=2, c=16)
 
 
 def tile_attend_gatedvalues_pl_kernel(tc, query, keys_words, keys_scales, size, vals, gval, offs, out_0, out_1, out_2):
@@ -33,59 +40,84 @@ def tile_attend_gatedvalues_pl_kernel(tc, query, keys_words, keys_scales, size, 
         slabs = ctx.enter_context(tc.tile_pool(name="slabs", bufs=1))
         psum = ctx.enter_context(tc.psum_pool(name="psum", bufs=2))
 
-        key_pool = keep.tile([P, T], U16, name="key_pool", align_bytes=64)
-        nc.sync.dma_start(key_pool[:].bitcast(I32), keys_words[0].bitcast(I32))
+        key_pool = slabs.tile([P, T], U16, name="key_pool", offset=3 * SLAB_BYTES - 2048, align_bytes=64)
         offsets = keep.tile([P, I // 16], U16, name="offsets")
         nc.sync.dma_start(offsets[:], offs)
-        key_scale_pool = keep.tile([P, T], U8, name="key_scale_pool", align_bytes=64)
+        nc.sync.dma_start(key_pool[:].bitcast(I32), keys_words[0].bitcast(I32))
+        size_rows = keep.tile([P, P], F32, name="size_rows")
+        nc.vector.memset(size_rows[:], 0.0)
+        nc.sync.dma_start(size_rows[0:PACK, :], size.rearrange("o (j k) -> (o j) k", k=P))
+        key_scale_pool = slabs.tile([P, T], U8, name="key_scale_pool", offset=8 * SLAB_BYTES + 4096, align_bytes=64)
         nc.gpsimd.memset(key_scale_pool[:].bitcast(I32), 0)
-        for quad in range(4):
-            nc.sync.dma_start(
-                key_scale_pool[32 * quad : 32 * quad + 4, :].bitcast(I32),
-                keys_scales[0, 4 * quad : 4 * quad + 4, :].bitcast(I32),
-            )
-        slot_size = keep.tile([P, PACK], F32, name="slot_size")
-        nc.scalar.dma_start(slot_size[:], size.rearrange("o (s r) -> (o s) r", r=PACK))
-
+        nc.sync.dma_start(key_scale_pool[32:96:4, :].bitcast(I32), keys_scales[0].bitcast(I32))
         warm_in = keep.tile([P, 1], F32, name="warm_in")
         warm_out = keep.tile([P, 1], F32, name="warm_out")
         nc.vector.memset(warm_in[:], 0.0)
         nc.scalar.activation(warm_out[:], warm_in[:], ACT.Exp)
-
-        q_raw = keep.tile([P, PACK, Q], F32, name="q_raw")
+        q_raw = slabs.tile([P, PACK, Q], F32, name="q_raw", offset=5 * SLAB_BYTES - 2048, align_bytes=64)
         nc.sync.dma_start(q_raw[:], query.rearrange("(p j) q -> p j q", j=PACK))
 
-        gate_rows = gval.rearrange("(p t) c -> t p c", t=PACK)
-        value_rows = vals.rearrange("(p t) c -> t p c", t=PACK)
-        slab_rows = [gate_rows[t] for t in range(PACK)] + [value_rows[t] for t in range(PACK)]
-        pools = []
-        for n in range(SLABS):
-            pools.append(slabs.tile([P, T], F32, name="pool%d" % n, offset=n * SLAB_BYTES))
-            nc.sync.dma_start(pools[n][:], slab_rows[n])
+        gate_rows = gval.rearrange("(p t) c -> p (t c)", t=PACK)
+        value_rows = vals.rearrange("(p t) c -> p (t c)", t=PACK)
+        windows = []
 
+        def load(rows, first, count):
+            at = len(windows)
+            pool = slabs.tile([P, count * T], F32, name="pool%d" % at, offset=at * SLAB_BYTES, align_bytes=64)
+            nc.sync.dma_start(pool[:], rows[:, first * T : (first + count) * T])
+            windows.extend(pool[:, n * T : (n + 1) * T] for n in range(count))
+
+        load(gate_rows, 0, 1)
+        load(gate_rows, 1, 1)
         ident = keep.tile([P, P], F32, name="ident")
         make_identity(nc, ident[:])
 
-        key_words = keep.tile([P, I], U16, name="key_words", align_bytes=64)
+        key_words = slabs.tile([P, I], U16, name="key_words", offset=8 * SLAB_BYTES + 4096, align_bytes=64)
         key_scales = keep.tile([P, I], U8, name="key_scales", align_bytes=64)
+        picked_scales = keep.tile([P, I], U8, name="picked_scales", align_bytes=64)
+        nc.vector.memset(key_scales[:].bitcast(I32), 0)
+        nc.vector.tensor_copy(picked_scales[:], key_scale_pool[:].indirect(offsets[:]))
         nc.vector.tensor_copy(key_words[:], key_pool[:].indirect(offsets[:]))
-        nc.vector.tensor_copy(key_scales[:], key_scale_pool[:].indirect(offsets[:]))
+        for quad in range(4):
+            nc.scalar.dma_start(
+                key_scales[32 * quad : 32 * quad + 4, :].bitcast(I32),
+                picked_scales[32 + 16 * quad : 48 + 16 * quad : 4, :].bitcast(I32),
+            )
 
-        q_bf = keep.tile([P, Q, PACK], BF16, name="q_bf", align_bytes=64)
+        q_bf = slabs.tile([P, Q, PACK], BF16, name="q_bf", offset=7 * SLAB_BYTES - 1024, align_bytes=64)
         nc.scalar.copy(
             q_bf[:].rearrange("p (c i) j -> p c j i", i=4),
             q_raw[:].rearrange("p j (c i) -> p c j i", i=4),
         )
-        q_codes = keep.tile([P, Q], U32, name="q_codes", align_bytes=64)
+        q_codes = slabs.tile([P, Q], U32, name="q_codes", offset=8 * SLAB_BYTES + 2048, align_bytes=64)
         q_scales = keep.tile([P, Q], U8, name="q_scales", align_bytes=64)
         nc.vector.quantize_mx(q_codes[:].bitcast(FP8X4), q_scales[:], q_bf[:].rearrange("p q j -> p (q j)"))
+        load(gate_rows, 2, 1)
+        load(gate_rows, 3, 1)
+        for t in range(PACK):
+            load(value_rows, t, 1)
+
+        size_turned = psum.tile([P, P], F32, name="softmax_bank")
+        nc.tensor.transpose(size_turned[:], size_rows[:], ident[:])
+        size_cols = keep.tile([P, PACK], F32, name="size_cols")
+        nc.scalar.copy(size_cols[:], size_turned[:, 0:PACK])
+        size_spread = psum.tile([P, I], F32, name="softmax_bank")
+        for j in range(PACK):
+            nc.tensor.transpose(
+                size_spread[:, j * P : (j + 1) * P], size_cols[:, j : j + 1].to_broadcast([P, P]), ident[:]
+            )
+        slot_size = keep.tile([P, I], F32, name="slot_size")
+        nc.scalar.activation(dealt(slot_size[:]), listed(size_spread[:]), ACT.Copy, scale=0.5)
+
+        def turn(rows_bf, turned):
+            words = rows_bf.bitcast(F32)
+            for u in range(2):
+                nc.tensor.transpose(turned[:, u, :], words[:, u * P : (u + 1) * P], ident[:])
 
         def pick_and_turn(n, turned):
-            picked = ring.tile([P, I], BF16, name="picked", align_bytes=64)
-            nc.vector.tensor_copy(picked[:], pools[n][:].indirect(offsets[:]))
-            pairs = picked[:].bitcast(F32)
-            for u in range(2):
-                nc.tensor.transpose(turned[:, u, :], pairs[:, u::2], ident[:])
+            picked = ring.tile([P, I], BF16, name="picked", bufs=4, align_bytes=64)
+            nc.vector.tensor_copy(dealt(picked[:]), windows[n].indirect(offsets[:]))
+            turn(picked[:], turned)
 
         def regroup(turned, grouped):
             nc.scalar.copy(
@@ -99,10 +131,15 @@ def tile_attend_gatedvalues_pl_kernel(tc, query, keys_words, keys_scales, size, 
             nc.vector.quantize_mx(codes.bitcast(FP8X4), scales[:], grouped)
             return codes, scales[:]
 
+        def pick_pair(k):
+            turned = psum.tile([P, 2, 2, P], F32, name="turned")
+            for n in range(2):
+                pick_and_turn(2 * k + n, turned[:, n])
+            return turned
+
         planes = []
-        scores, neg_max, prob = [], [], []
-        row_sum = keep.tile([P, HALVES], F32, name="row_sum")
-        inv_sum = keep.tile([P, HALVES], F32, name="inv_sum")
+        first_turned = pick_pair(0)
+        scores = []
         for h in range(HALVES):
             cols = slice(h * P, (h + 1) * P)
             scores.append(psum.tile([P, I], F32, name="softmax_bank"))
@@ -112,25 +149,27 @@ def tile_attend_gatedvalues_pl_kernel(tc, query, keys_words, keys_scales, size, 
                 rhs=key_words[:].bitcast(FP4X4), rhs_scale=key_scales[:],
                 start=True, stop=True,
             )
+        neg_max = slabs.tile([P, HALVES], F32, name="neg_max", offset=SLAB_BYTES, align_bytes=64)
+        row_sum = keep.tile([P, HALVES], F32, name="row_sum")
+        inv_sum = keep.tile([P, HALVES], F32, name="inv_sum")
+        prob = keep.tile([P, HALVES, I], F32, name="prob")
         for h in range(HALVES):
-            neg_max.append(keep.tile([P, 1], F32, name="neg_max%d" % h))
-            nc.vector.tensor_reduce(neg_max[h][:], scores[h][:], AXIS.X, ALU.max, negate=True)
-            prob.append(keep.tile([P, PACK, P], F32, name="prob%d" % h))
+            nc.vector.tensor_reduce(neg_max[:, h : h + 1], scores[h][:], AXIS.X, ALU.max, negate=True)
             nc.scalar.activation(
-                prob[h][:], scores[h][:].rearrange("p (s r) -> p r s", r=PACK), ACT.Exp,
-                bias=neg_max[h][:], accum_out=row_sum[:, h : h + 1],
+                dealt(prob[:, h, :]), listed(scores[h][:]), ACT.Exp,
+                bias=neg_max[:, h : h + 1], accum_out=row_sum[:, h : h + 1],
             )
-        turned = psum.tile([P, 2, 2, P], F32, name="turned")
-        pick_and_turn(0, turned[:, 0])
-        pick_and_turn(1, turned[:, 1])
         nc.vector.reciprocal(inv_sum[:], row_sum[:])
-        by_slot = []
+        w_turned = psum.tile([P, 2, 2, P], F32, name="softmax_bank")
         for h in range(HALVES):
-            normed = keep.tile([P, PACK, P], F32, name="normed%d" % h)
-            nc.scalar.activation(normed[:], prob[h][:], ACT.Copy, scale=inv_sum[:, h : h + 1])
-            by_slot.append(psum.tile([P, PACK, P], F32, name="softmax_bank"))
-            for r in range(PACK):
-                nc.tensor.transpose(by_slot[h][:, r, :], normed[:, r, :], ident[:])
+            w_rows = keep.tile([P, I], BF16, name="w_rows%d" % h, align_bytes=64)
+            nc.vector.scalar_tensor_tensor(
+                w_rows[:], prob[:, h, :], inv_sum[:, h : h + 1], slot_size[:], ALU.mult, ALU.mult
+            )
+            turn(w_rows[:], w_turned[:, h])
+        first_grouped = slabs.tile([P, 2, 2 * I], BF16, name="first_grouped", offset=SLAB_BYTES, align_bytes=64)
+        regroup(first_turned[:], first_grouped[:, 1, :])
+        regroup(w_turned[:], first_grouped[:, 0, :])
 
         def weighted_sum(acc, operand, n, rows=slice(0, Q)):
             codes, scales = operand
@@ -149,46 +188,29 @@ def tile_attend_gatedvalues_pl_kernel(tc, query, keys_words, keys_scales, size, 
             return sums
 
         def sigmoid(gate, gate_sum):
-            half_tanh = ring.tile([P, 2, Q], F32, name="half_tanh")
-            nc.scalar.activation(half_tanh[:], gate_sum, ACT.Tanh, scale=0.5)
-            nc.scalar.activation(gate, half_tanh[:], ACT.Copy, scale=0.5, bias=0.5)
+            nc.scalar.activation(gate, gate_sum, ACT.Tanh)
+
+        def gated(y, half_sum, gate):
+            nc.vector.scalar_tensor_tensor(y, gate, 1.0, half_sum, ALU.add, ALU.mult)
 
         y_rows = out_0.rearrange("(p t) q -> p t q", t=PACK)
         gates = keep.tile([P, PACK, Q], F32, name="gates")
-        w_scales = keep.tile([P, Q], U8, name="w_scales", align_bytes=64)
-
-        operands = []
-        for k in range(3):
-            grouped = ring.tile([P, 2 * I], BF16, name="grouped", align_bytes=64)
-            regroup(turned[:], grouped[:])
-            turned = psum.tile([P, 2, 2, P], F32, name="turned")
-            pick_and_turn(2 * k + 2, turned[:, 0])
-            reuse = (2 * k + 2) * SLAB_BYTES
-            codes = slabs.tile([P, 2 * P], U32, name="codes%d" % k, offset=reuse, align_bytes=64)
-            operands.append(quantise(grouped[:], codes[:]))
-            if k == 0:
-                w_bf = slabs.tile([P, Q, PACK], BF16, name="w_bf", offset=reuse + 2048, align_bytes=64)
-                nc.vector.tensor_tensor(
-                    w_bf[:, 0:P, :],
-                    by_slot[0][:].rearrange("p r q -> p q r"),
-                    slot_size[:].unsqueeze(1).to_broadcast([P, P, PACK]),
-                    ALU.mult,
-                )
-                w_rows = keep.tile([P, PACK, P], BF16, name="w_rows")
-                for r in range(PACK):
-                    nc.scalar.activation(w_rows[:, r, :], by_slot[1][:, r, :], ACT.Copy, scale=slot_size[:, r : r + 1])
-                nc.scalar.copy(
-                    w_bf[:, P:Q, :].rearrange("p (c i) r -> p c r i", i=4),
-                    w_rows[:].rearrange("p r (c i) -> p c r i", i=4),
-                )
-            if k < 2:
-                pick_and_turn(2 * k + 3, turned[:, 1])
-            if k == 0:
-                w_codes = slabs.tile([P, Q], U32, name="w_codes", offset=reuse + SLAB_BYTES, align_bytes=64)
-                nc.vector.quantize_mx(w_codes[:].bitcast(FP8X4), w_scales[:], w_bf[:].rearrange("p q j -> p (q j)"))
-            if k < 2:
-                sigmoid(gates[:, 2 * k : 2 * k + 2, :], pair_sums(operands[k], "gate_sum")[:])
-        first_sums = pair_sums(operands[2], "value_sum")
+        turned = pick_pair(1)
+        grouped = ring.tile([P, 2 * I], BF16, name="grouped", align_bytes=64)
+        regroup(turned[:], grouped[:])
+        codes = slabs.tile([P, 2 * Q], U32, name="first_codes", offset=4 * SLAB_BYTES + 1024, align_bytes=64)
+        codes, scales = quantise(first_grouped[:].rearrange("p n c -> p (n c)"), codes[:])
+        w_codes, w_scales = codes[:, 0:Q], scales[:, 0:Q]
+        sigmoid(gates[:, 0:2, :], pair_sums((codes[:, Q:], scales[:, Q:]), "gate_sum")[:])
+        turned = pick_pair(2)
+        codes = slabs.tile([P, 2 * P], U32, name="codes23", offset=4 * SLAB_BYTES, align_bytes=64)
+        sigmoid(gates[:, 2:4, :], pair_sums(quantise(grouped[:], codes[:]), "gate_sum")[:])
+        grouped = ring.tile([P, 2 * I], BF16, name="grouped", align_bytes=64)
+        regroup(turned[:], grouped[:])
+        turned = psum.tile([P, 1, 2, P], F32, name="turned")
+        pick_and_turn(6, turned[:, 0])
+        codes = slabs.tile([P, 2 * P], U32, name="codes45", offset=6 * SLAB_BYTES, align_bytes=64)
+        first_sums = pair_sums(quantise(grouped[:], codes[:]), "value_sum")
 
         grouped = ring.tile([P, I], BF16, name="grouped", align_bytes=64)
         regroup(turned[:, 0:1], grouped[:])
@@ -198,23 +220,23 @@ def tile_attend_gatedvalues_pl_kernel(tc, query, keys_words, keys_scales, size, 
         value_sum = psum.tile([P, Q], F32, name="value_sum")
         weighted_sum(value_sum[:], quantise(grouped[:], codes[:]), 0)
         y_first = slabs.tile([P, 2, Q], F32, name="y_first", offset=7 * SLAB_BYTES + 2048)
-        nc.vector.tensor_tensor(y_first[:], first_sums[:], gates[:, 0:2, :], ALU.mult)
+        gated(y_first[:], first_sums[:], gates[:, 0:2, :])
         nc.sync.dma_start(y_rows[:, 0:2, :], y_first[:])
-        grouped = slabs.tile([P, I], BF16, name="grouped7", offset=SLABS * SLAB_BYTES, align_bytes=64)
+        grouped = slabs.tile([P, I], BF16, name="grouped7", offset=8 * SLAB_BYTES, align_bytes=64)
         regroup(turned[:], grouped[:])
         y_bf = keep.tile([P, Q, PACK], BF16, name="y_bf", align_bytes=64)
         nc.scalar.copy(y_bf[:, :, 0:2], y_first[:].rearrange("p t q -> p q t"))
         codes = keep.tile([P, P], U32, name="codes7", align_bytes=64)
         operand = quantise(grouped[:], codes[:])
         halves = [slice(h * P, (h + 1) * P) for h in range(HALVES)]
-        last_sums = [psum.tile([P, P], F32, name=name) for name in ("gate_sum", "gate_sum")]
+        last_sums = [psum.tile([P, P], F32, name="gate_sum") for h in range(HALVES)]
         for h in range(HALVES):
             weighted_sum(last_sums[h][:], operand, 0, halves[h])
-        y_last = slabs.tile([P, 2, Q], F32, name="y_last", offset=SLABS * SLAB_BYTES)
-        nc.vector.tensor_tensor(y_last[:, 0, :], value_sum[:], gates[:, 2, :], ALU.mult)
+        y_last = slabs.tile([P, 2, Q], F32, name="y_last", offset=8 * SLAB_BYTES)
+        gated(y_last[:, 0, :], value_sum[:], gates[:, 2, :])
         nc.sync.dma_start(y_rows[:, 2, :], y_last[:, 0, :])
         for h in range(HALVES):
-            nc.vector.tensor_tensor(y_last[:, 1, halves[h]], last_sums[h][:], gates[:, 3, halves[h]], ALU.mult)
+            gated(y_last[:, 1, halves[h]], last_sums[h][:], gates[:, 3, halves[h]])
         nc.scalar.dma_start(y_rows[:, 3, :], y_last[:, 1, :])
         for h in range(HALVES):
             nc.vector.tensor_copy(y_bf[:, halves[h], 2:4], y_last[:, :, halves[h]].rearrange("p t q -> p q t"))

@@ -50,10 +50,6 @@ def tile_attend_gatedvalues_pl_kernel(tc, query, keys_words, keys_scales, size, 
         key_scale_pool = slabs.tile([P, T], U8, name="key_scale_pool", offset=8 * SLAB_BYTES + 4096, align_bytes=64)
         nc.gpsimd.memset(key_scale_pool[:].bitcast(I32), 0)
         nc.sync.dma_start(key_scale_pool[32:96:4, :].bitcast(I32), keys_scales[0].bitcast(I32))
-        warm_in = keep.tile([P, 1], F32, name="warm_in")
-        warm_out = keep.tile([P, 1], F32, name="warm_out")
-        nc.vector.memset(warm_in[:], 0.0)
-        nc.scalar.activation(warm_out[:], warm_in[:], ACT.Exp)
         q_raw = slabs.tile([P, PACK, Q], F32, name="q_raw", offset=5 * SLAB_BYTES - 2048, align_bytes=64)
         nc.sync.dma_start(q_raw[:], query.rearrange("(p j) q -> p j q", j=PACK))
 

@@ -40,17 +40,25 @@ def tile_attend_gatedvalues_pl_kernel(tc, query, keys_words, keys_scales, size, 
         slabs = ctx.enter_context(tc.tile_pool(name="slabs", bufs=1))
         psum = ctx.enter_context(tc.psum_pool(name="psum", bufs=2))
 
-        key_pool = slabs.tile([P, T], U16, name="key_pool", offset=3 * SLAB_BYTES - 2048, align_bytes=64)
+        key_pool = keep.tile([P, T], U16, name="key_pool", align_bytes=64)
         offsets = keep.tile([P, I // 16], U16, name="offsets")
         nc.sync.dma_start(offsets[:], offs)
         nc.sync.dma_start(key_pool[:].bitcast(I32), keys_words[0].bitcast(I32))
         size_rows = keep.tile([P, P], F32, name="size_rows")
         nc.vector.memset(size_rows[:], 0.0)
         nc.sync.dma_start(size_rows[0:PACK, :], size.rearrange("o (j k) -> (o j) k", k=P))
-        key_scale_pool = slabs.tile([P, T], U8, name="key_scale_pool", offset=8 * SLAB_BYTES + 4096, align_bytes=64)
+        key_scale_pool = keep.tile([P, T], U8, name="key_scale_pool", align_bytes=64)
         nc.gpsimd.memset(key_scale_pool[:].bitcast(I32), 0)
-        nc.sync.dma_start(key_scale_pool[32:96:4, :].bitcast(I32), keys_scales[0].bitcast(I32))
-        q_raw = slabs.tile([P, PACK, Q], F32, name="q_raw", offset=5 * SLAB_BYTES - 2048, align_bytes=64)
+        for quad in range(4):
+            nc.sync.dma_start(
+                key_scale_pool[32 * quad : 32 * quad + 4, :].bitcast(I32),
+                keys_scales[0, 4 * quad : 4 * quad + 4, :].bitcast(I32),
+            )
+        warm_in = keep.tile([P, 1], F32, name="warm_in")
+        warm_out = keep.tile([P, 1], F32, name="warm_out")
+        nc.vector.memset(warm_in[:], 0.0)
+        nc.scalar.activation(warm_out[:], warm_in[:], ACT.Exp)
+        q_raw = keep.tile([P, PACK, Q], F32, name="q_raw")
         nc.sync.dma_start(q_raw[:], query.rearrange("(p j) q -> p j q", j=PACK))
 
         gate_rows = gval.rearrange("(p t) c -> p (t c)", t=PACK)
@@ -68,19 +76,12 @@ def tile_attend_gatedvalues_pl_kernel(tc, query, keys_words, keys_scales, size, 
         ident = keep.tile([P, P], F32, name="ident")
         make_identity(nc, ident[:])
 
-        key_words = slabs.tile([P, I], U16, name="key_words", offset=8 * SLAB_BYTES + 4096, align_bytes=64)
+        key_words = keep.tile([P, I], U16, name="key_words", align_bytes=64)
         key_scales = keep.tile([P, I], U8, name="key_scales", align_bytes=64)
-        picked_scales = keep.tile([P, I], U8, name="picked_scales", align_bytes=64)
-        nc.vector.memset(key_scales[:].bitcast(I32), 0)
-        nc.vector.tensor_copy(picked_scales[:], key_scale_pool[:].indirect(offsets[:]))
         nc.vector.tensor_copy(key_words[:], key_pool[:].indirect(offsets[:]))
-        for quad in range(4):
-            nc.scalar.dma_start(
-                key_scales[32 * quad : 32 * quad + 4, :].bitcast(I32),
-                picked_scales[32 + 16 * quad : 48 + 16 * quad : 4, :].bitcast(I32),
-            )
+        nc.vector.tensor_copy(key_scales[:], key_scale_pool[:].indirect(offsets[:]))
 
-        q_bf = slabs.tile([P, Q, PACK], BF16, name="q_bf", offset=7 * SLAB_BYTES - 1024, align_bytes=64)
+        q_bf = keep.tile([P, Q, PACK], BF16, name="q_bf", align_bytes=64)
         nc.scalar.copy(
             q_bf[:].rearrange("p (c i) j -> p c j i", i=4),
             q_raw[:].rearrange("p j (c i) -> p c j i", i=4),
@@ -103,7 +104,7 @@ def tile_attend_gatedvalues_pl_kernel(tc, query, keys_words, keys_scales, size, 
                 size_spread[:, j * P : (j + 1) * P], size_cols[:, j : j + 1].to_broadcast([P, P]), ident[:]
             )
         slot_size = keep.tile([P, I], F32, name="slot_size")
-        nc.scalar.activation(dealt(slot_size[:]), listed(size_spread[:]), ACT.Copy, scale=0.5)
+        nc.scalar.copy(dealt(slot_size[:]), listed(size_spread[:]))
 
         def turn(rows_bf, turned):
             words = rows_bf.bitcast(F32)
@@ -145,7 +146,7 @@ def tile_attend_gatedvalues_pl_kernel(tc, query, keys_words, keys_scales, size, 
                 rhs=key_words[:].bitcast(FP4X4), rhs_scale=key_scales[:],
                 start=True, stop=True,
             )
-        neg_max = slabs.tile([P, HALVES], F32, name="neg_max", offset=SLAB_BYTES, align_bytes=64)
+        neg_max = slabs.tile([P, HALVES], F32, name="neg_max", offset=0, align_bytes=64)
         row_sum = keep.tile([P, HALVES], F32, name="row_sum")
         inv_sum = keep.tile([P, HALVES], F32, name="inv_sum")
         prob = keep.tile([P, HALVES, I], F32, name="prob")
@@ -163,7 +164,7 @@ def tile_attend_gatedvalues_pl_kernel(tc, query, keys_words, keys_scales, size, 
                 w_rows[:], prob[:, h, :], inv_sum[:, h : h + 1], slot_size[:], ALU.mult, ALU.mult
             )
             turn(w_rows[:], w_turned[:, h])
-        first_grouped = slabs.tile([P, 2, 2 * I], BF16, name="first_grouped", offset=SLAB_BYTES, align_bytes=64)
+        first_grouped = slabs.tile([P, 2, 2 * I], BF16, name="first_grouped", offset=0, align_bytes=64)
         regroup(first_turned[:], first_grouped[:, 1, :])
         regroup(w_turned[:], first_grouped[:, 0, :])
 
@@ -184,17 +185,19 @@ def tile_attend_gatedvalues_pl_kernel(tc, query, keys_words, keys_scales, size, 
             return sums
 
         def sigmoid(gate, gate_sum):
-            nc.scalar.activation(gate, gate_sum, ACT.Tanh)
+            half_tanh = ring.tile([P, 2, Q], F32, name="half_tanh")
+            nc.scalar.activation(half_tanh[:], gate_sum, ACT.Tanh, scale=0.5)
+            nc.scalar.activation(gate, half_tanh[:], ACT.Copy, scale=0.5, bias=0.5)
 
         def gated(y, half_sum, gate):
-            nc.vector.scalar_tensor_tensor(y, gate, 1.0, half_sum, ALU.add, ALU.mult)
+            nc.vector.tensor_tensor(y, half_sum, gate, ALU.mult)
 
         y_rows = out_0.rearrange("(p t) q -> p t q", t=PACK)
         gates = keep.tile([P, PACK, Q], F32, name="gates")
         turned = pick_pair(1)
         grouped = ring.tile([P, 2 * I], BF16, name="grouped", align_bytes=64)
         regroup(turned[:], grouped[:])
-        codes = slabs.tile([P, 2 * Q], U32, name="first_codes", offset=4 * SLAB_BYTES + 1024, align_bytes=64)
+        codes = slabs.tile([P, 2 * Q], U32, name="first_codes", offset=3 * SLAB_BYTES, align_bytes=64)
         codes, scales = quantise(first_grouped[:].rearrange("p n c -> p (n c)"), codes[:])
         w_codes, w_scales = codes[:, 0:Q], scales[:, 0:Q]
         sigmoid(gates[:, 0:2, :], pair_sums((codes[:, Q:], scales[:, Q:]), "gate_sum")[:])

@@ -42,11 +42,8 @@ def tile_attend_gatedvalues_pl_kernel(tc, query, keys_words, keys_scales, size, 
 
         key_pool = keep.tile([P, T], U16, name="key_pool", align_bytes=64)
         offsets = keep.tile([P, I // 16], U16, name="offsets")
-        nc.sync.dma_start(offsets[:], offs)
         nc.sync.dma_start(key_pool[:].bitcast(I32), keys_words[0].bitcast(I32))
-        size_rows = keep.tile([P, P], F32, name="size_rows")
-        nc.vector.memset(size_rows[:], 0.0)
-        nc.sync.dma_start(size_rows[0:PACK, :], size.rearrange("o (j k) -> (o j) k", k=P))
+        nc.sync.dma_start(offsets[:], offs)
         key_scale_pool = keep.tile([P, T], U8, name="key_scale_pool", align_bytes=64)
         nc.gpsimd.memset(key_scale_pool[:].bitcast(I32), 0)
         for quad in range(4):
@@ -54,6 +51,9 @@ def tile_attend_gatedvalues_pl_kernel(tc, query, keys_words, keys_scales, size, 
                 key_scale_pool[32 * quad : 32 * quad + 4, :].bitcast(I32),
                 keys_scales[0, 4 * quad : 4 * quad + 4, :].bitcast(I32),
             )
+        size_rows = keep.tile([P, P], F32, name="size_rows")
+        nc.gpsimd.memset(size_rows[:], 0.0)
+        nc.gpsimd.dma_start(size_rows[0:PACK, :], size.rearrange("o (j k) -> (o j) k", k=P))
         warm_in = keep.tile([P, 1], F32, name="warm_in")
         warm_out = keep.tile([P, 1], F32, name="warm_out")
         nc.vector.memset(warm_in[:], 0.0)
@@ -94,11 +94,11 @@ def tile_attend_gatedvalues_pl_kernel(tc, query, keys_words, keys_scales, size, 
         for t in range(PACK):
             load(value_rows, t, 1)
 
-        size_turned = psum.tile([P, P], F32, name="softmax_bank")
+        size_turned = psum.tile([P, P], F32, name="value_sum")
         nc.tensor.transpose(size_turned[:], size_rows[:], ident[:])
         size_cols = keep.tile([P, PACK], F32, name="size_cols")
         nc.scalar.copy(size_cols[:], size_turned[:, 0:PACK])
-        size_spread = psum.tile([P, I], F32, name="softmax_bank")
+        size_spread = psum.tile([P, I], F32, name="value_sum")
         for j in range(PACK):
             nc.tensor.transpose(
                 size_spread[:, j * P : (j + 1) * P], size_cols[:, j : j + 1].to_broadcast([P, P]), ident[:]

@@ -51,13 +51,8 @@ def tile_attend_gatedvalues_pl_kernel(tc, query, keys_words, keys_scales, size, 
                 key_scale_pool[32 * quad : 32 * quad + 4, :].bitcast(I32),
                 keys_scales[0, 4 * quad : 4 * quad + 4, :].bitcast(I32),
             )
-        size_rows = keep.tile([P, P], F32, name="size_rows")
-        nc.gpsimd.memset(size_rows[:], 0.0)
-        nc.gpsimd.dma_start(size_rows[0:PACK, :], size.rearrange("o (j k) -> (o j) k", k=P))
-        warm_in = keep.tile([P, 1], F32, name="warm_in")
-        warm_out = keep.tile([P, 1], F32, name="warm_out")
-        nc.vector.memset(warm_in[:], 0.0)
-        nc.scalar.activation(warm_out[:], warm_in[:], ACT.Exp)
+        size_cols = keep.tile([P, PACK], F32, name="size_cols")
+        nc.scalar.dma_start(size_cols[:], size.rearrange("o (s r) -> (o s) r", r=PACK))
         q_raw = keep.tile([P, PACK, Q], F32, name="q_raw")
         nc.sync.dma_start(q_raw[:], query.rearrange("(p j) q -> p j q", j=PACK))
 
@@ -72,7 +67,6 @@ def tile_attend_gatedvalues_pl_kernel(tc, query, keys_words, keys_scales, size, 
             windows.extend(pool[:, n * T : (n + 1) * T] for n in range(count))
 
         load(gate_rows, 0, 1)
-        load(gate_rows, 1, 1)
         ident = keep.tile([P, P], F32, name="ident")
         make_identity(nc, ident[:])
 
@@ -89,22 +83,23 @@ def tile_attend_gatedvalues_pl_kernel(tc, query, keys_words, keys_scales, size, 
         q_codes = slabs.tile([P, Q], U32, name="q_codes", offset=8 * SLAB_BYTES + 2048, align_bytes=64)
         q_scales = keep.tile([P, Q], U8, name="q_scales", align_bytes=64)
         nc.vector.quantize_mx(q_codes[:].bitcast(FP8X4), q_scales[:], q_bf[:].rearrange("p q j -> p (q j)"))
+        load(gate_rows, 1, 1)
         load(gate_rows, 2, 1)
         load(gate_rows, 3, 1)
         for t in range(PACK):
             load(value_rows, t, 1)
 
-        size_turned = psum.tile([P, P], F32, name="value_sum")
-        nc.tensor.transpose(size_turned[:], size_rows[:], ident[:])
-        size_cols = keep.tile([P, PACK], F32, name="size_cols")
-        nc.scalar.copy(size_cols[:], size_turned[:, 0:PACK])
         size_spread = psum.tile([P, I], F32, name="value_sum")
         for j in range(PACK):
             nc.tensor.transpose(
                 size_spread[:, j * P : (j + 1) * P], size_cols[:, j : j + 1].to_broadcast([P, P]), ident[:]
             )
         slot_size = keep.tile([P, I], F32, name="slot_size")
-        nc.scalar.copy(dealt(slot_size[:]), listed(size_spread[:]))
+        nc.scalar.activation(
+            slot_size[:].rearrange("p (u g c r) -> p g u c r", u=2, c=4, r=PACK),
+            size_spread[:].rearrange("p (r g u c) -> p g u c r", r=PACK, u=2, c=4),
+            ACT.Copy, scale=0.5,
+        )
 
         def turn(rows_bf, turned):
             words = rows_bf.bitcast(F32)
@@ -112,7 +107,10 @@ def tile_attend_gatedvalues_pl_kernel(tc, query, keys_words, keys_scales, size, 
                 nc.tensor.transpose(turned[:, u, :], words[:, u * P : (u + 1) * P], ident[:])
 
         def pick_and_turn(n, turned):
-            picked = ring.tile([P, I], BF16, name="picked", bufs=4, align_bytes=64)
+            if n == 0:
+                picked = slabs.tile([P, I], BF16, name="picked0", offset=8 * SLAB_BYTES + 2048, align_bytes=64)
+            else:
+                picked = ring.tile([P, I], BF16, name="picked", bufs=4, align_bytes=64)
             nc.vector.tensor_copy(dealt(picked[:]), windows[n].indirect(offsets[:]))
             turn(picked[:], turned)
 
@@ -135,7 +133,6 @@ def tile_attend_gatedvalues_pl_kernel(tc, query, keys_words, keys_scales, size, 
             return turned
 
         planes = []
-        first_turned = pick_pair(0)
         scores = []
         for h in range(HALVES):
             cols = slice(h * P, (h + 1) * P)
@@ -146,7 +143,7 @@ def tile_attend_gatedvalues_pl_kernel(tc, query, keys_words, keys_scales, size, 
                 rhs=key_words[:].bitcast(FP4X4), rhs_scale=key_scales[:],
                 start=True, stop=True,
             )
-        neg_max = slabs.tile([P, HALVES], F32, name="neg_max", offset=0, align_bytes=64)
+        neg_max = slabs.tile([P, HALVES], F32, name="neg_max", offset=9 * SLAB_BYTES, align_bytes=64)
         row_sum = keep.tile([P, HALVES], F32, name="row_sum")
         inv_sum = keep.tile([P, HALVES], F32, name="inv_sum")
         prob = keep.tile([P, HALVES, I], F32, name="prob")
@@ -156,6 +153,7 @@ def tile_attend_gatedvalues_pl_kernel(tc, query, keys_words, keys_scales, size, 
                 dealt(prob[:, h, :]), listed(scores[h][:]), ACT.Exp,
                 bias=neg_max[:, h : h + 1], accum_out=row_sum[:, h : h + 1],
             )
+        first_turned = pick_pair(0)
         nc.vector.reciprocal(inv_sum[:], row_sum[:])
         w_turned = psum.tile([P, 2, 2, P], F32, name="softmax_bank")
         for h in range(HALVES):
@@ -164,7 +162,7 @@ def tile_attend_gatedvalues_pl_kernel(tc, query, keys_words, keys_scales, size, 
                 w_rows[:], prob[:, h, :], inv_sum[:, h : h + 1], slot_size[:], ALU.mult, ALU.mult
             )
             turn(w_rows[:], w_turned[:, h])
-        first_grouped = slabs.tile([P, 2, 2 * I], BF16, name="first_grouped", offset=0, align_bytes=64)
+        first_grouped = slabs.tile([P, 2, 2 * I], BF16, name="first_grouped", offset=9 * SLAB_BYTES, align_bytes=64)
         regroup(first_turned[:], first_grouped[:, 1, :])
         regroup(w_turned[:], first_grouped[:, 0, :])
 
@@ -185,12 +183,10 @@ def tile_attend_gatedvalues_pl_kernel(tc, query, keys_words, keys_scales, size, 
             return sums
 
         def sigmoid(gate, gate_sum):
-            half_tanh = ring.tile([P, 2, Q], F32, name="half_tanh")
-            nc.scalar.activation(half_tanh[:], gate_sum, ACT.Tanh, scale=0.5)
-            nc.scalar.activation(gate, half_tanh[:], ACT.Copy, scale=0.5, bias=0.5)
+            nc.scalar.activation(gate, gate_sum, ACT.Tanh)
 
         def gated(y, half_sum, gate):
-            nc.vector.tensor_tensor(y, half_sum, gate, ALU.mult)
+            nc.vector.scalar_tensor_tensor(y, gate, 1.0, half_sum, ALU.add, ALU.mult)
 
         y_rows = out_0.rearrange("(p t) q -> p t q", t=PACK)
         gates = keep.tile([P, PACK, Q], F32, name="gates")
@@ -218,27 +214,32 @@ def tile_attend_gatedvalues_pl_kernel(tc, query, keys_words, keys_scales, size, 
         codes = slabs.tile([P, P], U32, name="codes6", offset=7 * SLAB_BYTES, align_bytes=64)
         value_sum = psum.tile([P, Q], F32, name="value_sum")
         weighted_sum(value_sum[:], quantise(grouped[:], codes[:]), 0)
-        y_first = slabs.tile([P, 2, Q], F32, name="y_first", offset=7 * SLAB_BYTES + 2048)
-        gated(y_first[:], first_sums[:], gates[:, 0:2, :])
-        nc.sync.dma_start(y_rows[:, 0:2, :], y_first[:])
-        grouped = slabs.tile([P, I], BF16, name="grouped7", offset=8 * SLAB_BYTES, align_bytes=64)
-        regroup(turned[:], grouped[:])
+        y = slabs.tile([P, PACK, Q], F32, name="y", offset=7 * SLAB_BYTES + 2048, align_bytes=64)
+        gated(y[:, 0:2, :], first_sums[:], gates[:, 0:2, :])
+        nc.sync.dma_start(y_rows[:, 0:2, :], y[:, 0:2, :])
+        grouped = y[:, 2, :].bitcast(BF16)
+        regroup(turned[:], grouped)
         y_bf = keep.tile([P, Q, PACK], BF16, name="y_bf", align_bytes=64)
-        nc.scalar.copy(y_bf[:, :, 0:2], y_first[:].rearrange("p t q -> p q t"))
         codes = keep.tile([P, P], U32, name="codes7", align_bytes=64)
-        operand = quantise(grouped[:], codes[:])
+        operand = quantise(grouped, codes[:])
         halves = [slice(h * P, (h + 1) * P) for h in range(HALVES)]
         last_sums = [psum.tile([P, P], F32, name="gate_sum") for h in range(HALVES)]
         for h in range(HALVES):
             weighted_sum(last_sums[h][:], operand, 0, halves[h])
-        y_last = slabs.tile([P, 2, Q], F32, name="y_last", offset=8 * SLAB_BYTES)
-        gated(y_last[:, 0, :], value_sum[:], gates[:, 2, :])
-        nc.sync.dma_start(y_rows[:, 2, :], y_last[:, 0, :])
+        gated(y[:, 2, :], value_sum[:], gates[:, 2, :])
+        nc.sync.dma_start(y_rows[:, 2, :], y[:, 2, :])
         for h in range(HALVES):
-            gated(y_last[:, 1, halves[h]], last_sums[h][:], gates[:, 3, halves[h]])
-        nc.scalar.dma_start(y_rows[:, 3, :], y_last[:, 1, :])
-        for h in range(HALVES):
-            nc.vector.tensor_copy(y_bf[:, halves[h], 2:4], y_last[:, :, halves[h]].rearrange("p t q -> p q t"))
+            gated(y[:, 3, halves[h]], last_sums[h][:], gates[:, 3, halves[h]])
+        nc.scalar.dma_start(y_rows[:, 3, :], y[:, 3, :])
+        for copy, rows in (
+            (nc.scalar.copy, slice(0, P // 2)),
+            (nc.vector.tensor_copy, slice(P // 2, P)),
+            (nc.vector.tensor_copy, halves[1]),
+        ):
+            copy(
+                y_bf[:, rows, :].rearrange("p (c i) t -> p c t i", i=4),
+                y[:, :, rows].rearrange("p t (c i) -> p c t i", i=4),
+            )
 
         y_codes = keep.tile([P, Q], U32, name="y_codes", align_bytes=64)
         y_scales = keep.tile([P, Q], U8, name="y_scales", align_bytes=64)

@@ -191,21 +191,20 @@ def tile_attend_gatedvalues_pl_kernel(tc, query, keys_words, keys_scales, size, 
         y_rows = out_0.rearrange("(p t) q -> p t q", t=PACK)
         gates = keep.tile([P, PACK, Q], F32, name="gates")
         turned = pick_pair(1)
-        grouped = ring.tile([P, 2 * I], BF16, name="grouped", align_bytes=64)
-        regroup(turned[:], grouped[:])
+        late_grouped = keep.tile([P, 2, 2 * I], BF16, name="late_grouped", align_bytes=64)
+        regroup(turned[:], late_grouped[:, 0, :])
         codes = slabs.tile([P, 2 * Q], U32, name="first_codes", offset=3 * SLAB_BYTES, align_bytes=64)
         codes, scales = quantise(first_grouped[:].rearrange("p n c -> p (n c)"), codes[:])
         w_codes, w_scales = codes[:, 0:Q], scales[:, 0:Q]
         sigmoid(gates[:, 0:2, :], pair_sums((codes[:, Q:], scales[:, Q:]), "gate_sum")[:])
         turned = pick_pair(2)
-        codes = slabs.tile([P, 2 * P], U32, name="codes23", offset=4 * SLAB_BYTES, align_bytes=64)
-        sigmoid(gates[:, 2:4, :], pair_sums(quantise(grouped[:], codes[:]), "gate_sum")[:])
-        grouped = ring.tile([P, 2 * I], BF16, name="grouped", align_bytes=64)
-        regroup(turned[:], grouped[:])
+        regroup(turned[:], late_grouped[:, 1, :])
         turned = psum.tile([P, 1, 2, P], F32, name="turned")
         pick_and_turn(6, turned[:, 0])
-        codes = slabs.tile([P, 2 * P], U32, name="codes45", offset=6 * SLAB_BYTES, align_bytes=64)
-        first_sums = pair_sums(quantise(grouped[:], codes[:]), "value_sum")
+        codes = slabs.tile([P, 4 * P], U32, name="late_codes", offset=6 * SLAB_BYTES, align_bytes=64)
+        codes, scales = quantise(late_grouped[:].rearrange("p n c -> p (n c)"), codes[:])
+        sigmoid(gates[:, 2:4, :], pair_sums((codes, scales), "gate_sum")[:])
+        first_sums = pair_sums((codes[:, 2 * P :], scales[:, 2 * P :]), "value_sum")
 
         grouped = ring.tile([P, I], BF16, name="grouped", align_bytes=64)
         regroup(turned[:, 0:1], grouped[:])
@@ -227,10 +226,9 @@ def tile_attend_gatedvalues_pl_kernel(tc, query, keys_words, keys_scales, size, 
         for h in range(HALVES):
             weighted_sum(last_sums[h][:], operand, 0, halves[h])
         gated(y[:, 2, :], value_sum[:], gates[:, 2, :])
-        nc.sync.dma_start(y_rows[:, 2, :], y[:, 2, :])
         for h in range(HALVES):
             gated(y[:, 3, halves[h]], last_sums[h][:], gates[:, 3, halves[h]])
-        nc.scalar.dma_start(y_rows[:, 3, :], y[:, 3, :])
+        nc.sync.dma_start(y_rows[:, 2:4, :], y[:, 2:4, :])
         for copy, rows in (
             (nc.scalar.copy, slice(0, P // 2)),
             (nc.vector.tensor_copy, slice(P // 2, P)),
@@ -248,7 +246,10 @@ def tile_attend_gatedvalues_pl_kernel(tc, query, keys_words, keys_scales, size, 
                 y_codes[:, halves[h]].bitcast(FP8X4), y_scales[:, halves[h]],
                 y_bf[:, halves[h], :].rearrange("p q j -> p (q j)"),
             )
-        nc.sync.dma_start(out_1[0].rearrange("p q j -> p (q j)").bitcast(I32), y_codes[:].bitcast(I32))
+            queue = nc.scalar if h == 0 else nc.sync
+            queue.dma_start(
+                out_1[0, :, halves[h], :].rearrange("p q j -> p (q j)").bitcast(I32), y_codes[:, halves[h]].bitcast(I32)
+            )
         for quad in range(4):
             queue = nc.scalar if quad % 2 == 0 else nc.sync
             queue.dma_start(

@@ -22,14 +22,7 @@ P = 128
 PACK = 4
 HALVES = Q // P
 SLAB_BYTES = 4 * T
-
-
-def dealt(row):
-    return row.rearrange("p (u g c) -> p g u c", u=2, c=16)
-
-
-def listed(row):
-    return row.rearrange("p (g u c) -> p g u c", u=2, c=16)
+SPLIT = 256
 
 
 def tile_attend_gatedvalues_pl_kernel(tc, query, keys_words, keys_scales, size, vals, gval, offs, out_0, out_1, out_2):
@@ -96,22 +89,28 @@ def tile_attend_gatedvalues_pl_kernel(tc, query, keys_words, keys_scales, size, 
             )
         slot_size = keep.tile([P, I], F32, name="slot_size")
         nc.scalar.activation(
-            slot_size[:].rearrange("p (u g c r) -> p g u c r", u=2, c=4, r=PACK),
-            size_spread[:].rearrange("p (r g u c) -> p g u c r", r=PACK, u=2, c=4),
+            slot_size[:].rearrange("p (s r) -> p s r", r=PACK),
+            size_spread[:].rearrange("p (r s) -> p s r", r=PACK),
             ACT.Copy, scale=0.5,
         )
 
         def turn(rows_bf, turned):
             words = rows_bf.bitcast(F32)
             for u in range(2):
-                nc.tensor.transpose(turned[:, u, :], words[:, u * P : (u + 1) * P], ident[:])
+                nc.tensor.transpose(turned[:, u, :], words[:, u : 2 * P : 2], ident[:])
 
         def pick_and_turn(n, turned):
             if n == 0:
                 picked = slabs.tile([P, I], BF16, name="picked0", offset=8 * SLAB_BYTES + 2048, align_bytes=64)
             else:
                 picked = ring.tile([P, I], BF16, name="picked", bufs=4, align_bytes=64)
-            nc.vector.tensor_copy(dealt(picked[:]), windows[n].indirect(offsets[:]))
+            if n < 5:
+                nc.vector.tensor_copy(picked[:], windows[n].indirect(offsets[:]))
+            else:
+                nc.vector.tensor_copy(picked[:, 0:SPLIT], windows[n].indirect(offsets[:, 0 : SPLIT // 16]))
+                nc.scalar.activation(
+                    picked[:, SPLIT:I], windows[n].indirect(offsets[:, SPLIT // 16 : I // 16]), ACT.Copy
+                )
             turn(picked[:], turned)
 
         def regroup(turned, grouped):
@@ -150,7 +149,7 @@ def tile_attend_gatedvalues_pl_kernel(tc, query, keys_words, keys_scales, size, 
         for h in range(HALVES):
             nc.vector.tensor_reduce(neg_max[:, h : h + 1], scores[h][:], AXIS.X, ALU.max, negate=True)
             nc.scalar.activation(
-                dealt(prob[:, h, :]), listed(scores[h][:]), ACT.Exp,
+                prob[:, h, :], scores[h][:], ACT.Exp,
                 bias=neg_max[:, h : h + 1], accum_out=row_sum[:, h : h + 1],
             )
         first_turned = pick_pair(0)
@@ -189,22 +188,28 @@ def tile_attend_gatedvalues_pl_kernel(tc, query, keys_words, keys_scales, size, 
             nc.vector.scalar_tensor_tensor(y, gate, 1.0, half_sum, ALU.add, ALU.mult)
 
         y_rows = out_0.rearrange("(p t) q -> p t q", t=PACK)
-        gates = keep.tile([P, PACK, Q], F32, name="gates")
+        gates = keep.tile([P, 2, Q], F32, name="gates")
         turned = pick_pair(1)
-        late_grouped = keep.tile([P, 2, 2 * I], BF16, name="late_grouped", align_bytes=64)
+        late_grouped = keep.tile([P, 1, 2 * I], BF16, name="late_grouped", align_bytes=64)
+        value_grouped = keep.tile([P, 2 * I], BF16, name="value_grouped", align_bytes=64)
         regroup(turned[:], late_grouped[:, 0, :])
         codes = slabs.tile([P, 2 * Q], U32, name="first_codes", offset=3 * SLAB_BYTES, align_bytes=64)
         codes, scales = quantise(first_grouped[:].rearrange("p n c -> p (n c)"), codes[:])
         w_codes, w_scales = codes[:, 0:Q], scales[:, 0:Q]
-        sigmoid(gates[:, 0:2, :], pair_sums((codes[:, Q:], scales[:, Q:]), "gate_sum")[:])
-        turned = pick_pair(2)
-        regroup(turned[:], late_grouped[:, 1, :])
+        sigmoid(gates[:], pair_sums((codes[:, Q:], scales[:, Q:]), "gate_sum")[:])
+        for n in range(2):
+            turned = psum.tile([P, 1, 2, P], F32, name="turned")
+            pick_and_turn(4 + n, turned[:, 0])
+            regroup(turned[:], value_grouped[:, n * I : (n + 1) * I])
+            if n == 0:
+                codes = slabs.tile([P, 2 * P], U32, name="gate_codes", offset=4 * SLAB_BYTES, align_bytes=64)
+                late_gate_sums = pair_sums(quantise(late_grouped[:, 0, :], codes[:]), "gate_sum")
+        late_gates = slabs.tile([P, 2, Q], F32, name="late_gates", offset=5 * SLAB_BYTES, align_bytes=64)
+        sigmoid(late_gates[:], late_gate_sums[:])
         turned = psum.tile([P, 1, 2, P], F32, name="turned")
         pick_and_turn(6, turned[:, 0])
-        codes = slabs.tile([P, 4 * P], U32, name="late_codes", offset=6 * SLAB_BYTES, align_bytes=64)
-        codes, scales = quantise(late_grouped[:].rearrange("p n c -> p (n c)"), codes[:])
-        sigmoid(gates[:, 2:4, :], pair_sums((codes, scales), "gate_sum")[:])
-        first_sums = pair_sums((codes[:, 2 * P :], scales[:, 2 * P :]), "value_sum")
+        codes = slabs.tile([P, 2 * P], U32, name="late_codes", offset=6 * SLAB_BYTES, align_bytes=64)
+        first_sums = pair_sums(quantise(value_grouped[:], codes[:]), "value_sum")
 
         grouped = ring.tile([P, I], BF16, name="grouped", align_bytes=64)
         regroup(turned[:, 0:1], grouped[:])
@@ -214,7 +219,7 @@ def tile_attend_gatedvalues_pl_kernel(tc, query, keys_words, keys_scales, size, 
         value_sum = psum.tile([P, Q], F32, name="value_sum")
         weighted_sum(value_sum[:], quantise(grouped[:], codes[:]), 0)
         y = slabs.tile([P, PACK, Q], F32, name="y", offset=7 * SLAB_BYTES + 2048, align_bytes=64)
-        gated(y[:, 0:2, :], first_sums[:], gates[:, 0:2, :])
+        gated(y[:, 0:2, :], first_sums[:], gates[:])
         nc.sync.dma_start(y_rows[:, 0:2, :], y[:, 0:2, :])
         grouped = y[:, 2, :].bitcast(BF16)
         regroup(turned[:], grouped)
@@ -225,9 +230,9 @@ def tile_attend_gatedvalues_pl_kernel(tc, query, keys_words, keys_scales, size, 
         last_sums = [psum.tile([P, P], F32, name="gate_sum") for h in range(HALVES)]
         for h in range(HALVES):
             weighted_sum(last_sums[h][:], operand, 0, halves[h])
-        gated(y[:, 2, :], value_sum[:], gates[:, 2, :])
+        gated(y[:, 2, :], value_sum[:], late_gates[:, 0, :])
         for h in range(HALVES):
-            gated(y[:, 3, halves[h]], last_sums[h][:], gates[:, 3, halves[h]])
+            gated(y[:, 3, halves[h]], last_sums[h][:], late_gates[:, 1, halves[h]])
         nc.sync.dma_start(y_rows[:, 2:4, :], y[:, 2:4, :])
         for copy, rows in (
             (nc.scalar.copy, slice(0, P // 2)),

@@ -57,9 +57,9 @@ def tile_attend_gatedvalues_pl_kernel(tc, query, keys_words, keys_scales, size, 
             at = len(windows)
             pool = slabs.tile([P, count * T], F32, name="pool%d" % at, offset=at * SLAB_BYTES, align_bytes=64)
             nc.sync.dma_start(pool[:], rows[:, first * T : (first + count) * T])
-            windows.extend(pool[:, n * T : (n + 1) * T] for n in range(count))
+            windows.extend(pool[:, n * T :] for n in range(count))
 
-        load(gate_rows, 0, 1)
+        load(gate_rows, 0, 2)
         ident = keep.tile([P, P], F32, name="ident")
         make_identity(nc, ident[:])
 
@@ -73,12 +73,10 @@ def tile_attend_gatedvalues_pl_kernel(tc, query, keys_words, keys_scales, size, 
             q_bf[:].rearrange("p (c i) j -> p c j i", i=4),
             q_raw[:].rearrange("p j (c i) -> p c j i", i=4),
         )
-        q_codes = slabs.tile([P, Q], U32, name="q_codes", offset=8 * SLAB_BYTES + 2048, align_bytes=64)
+        q_codes = keep.tile([P, Q], U32, name="q_codes", align_bytes=64)
         q_scales = keep.tile([P, Q], U8, name="q_scales", align_bytes=64)
         nc.vector.quantize_mx(q_codes[:].bitcast(FP8X4), q_scales[:], q_bf[:].rearrange("p q j -> p (q j)"))
-        load(gate_rows, 1, 1)
-        load(gate_rows, 2, 1)
-        load(gate_rows, 3, 1)
+        load(gate_rows, 2, 2)
         for t in range(PACK):
             load(value_rows, t, 1)
 
@@ -101,10 +99,21 @@ def tile_attend_gatedvalues_pl_kernel(tc, query, keys_words, keys_scales, size, 
 
         def pick_and_turn(n, turned):
             if n == 0:
-                picked = slabs.tile([P, I], BF16, name="picked0", offset=8 * SLAB_BYTES + 2048, align_bytes=64)
+                picked = slabs.tile([P, I], BF16, name="picked0", offset=9 * SLAB_BYTES, align_bytes=64)
+            elif n == 3:
+                picked = slabs.tile([P, I], BF16, name="picked3", offset=8 * SLAB_BYTES, align_bytes=64)
             else:
                 picked = ring.tile([P, I], BF16, name="picked", bufs=4, align_bytes=64)
-            if n < 5:
+            if n in (0, 2):
+                nc.scalar.activation(picked[:], windows[n].indirect(offsets[:]), ACT.Copy)
+            elif n in (1, 3):
+                nc.vector.tensor_copy(
+                    picked[:].rearrange("p (u s c) -> p s u c", u=2, c=2), windows[n].indirect(offsets[:])
+                )
+                for u in range(2):
+                    nc.tensor.transpose(turned[:, u, :], picked[:].bitcast(F32)[:, u * P : (u + 1) * P], ident[:])
+                return
+            elif n == 4:
                 nc.vector.tensor_copy(picked[:], windows[n].indirect(offsets[:]))
             else:
                 nc.vector.tensor_copy(picked[:, 0:SPLIT], windows[n].indirect(offsets[:, 0 : SPLIT // 16]))
@@ -161,7 +170,7 @@ def tile_attend_gatedvalues_pl_kernel(tc, query, keys_words, keys_scales, size, 
                 w_rows[:], prob[:, h, :], inv_sum[:, h : h + 1], slot_size[:], ALU.mult, ALU.mult
             )
             turn(w_rows[:], w_turned[:, h])
-        first_grouped = slabs.tile([P, 2, 2 * I], BF16, name="first_grouped", offset=9 * SLAB_BYTES, align_bytes=64)
+        first_grouped = keep.tile([P, 2, 2 * I], BF16, name="first_grouped", align_bytes=64)
         regroup(first_turned[:], first_grouped[:, 1, :])
         regroup(w_turned[:], first_grouped[:, 0, :])
 
@@ -188,12 +197,12 @@ def tile_attend_gatedvalues_pl_kernel(tc, query, keys_words, keys_scales, size, 
             nc.vector.scalar_tensor_tensor(y, gate, 1.0, half_sum, ALU.add, ALU.mult)
 
         y_rows = out_0.rearrange("(p t) q -> p t q", t=PACK)
-        gates = keep.tile([P, 2, Q], F32, name="gates")
+        gates = slabs.tile([P, 2, Q], F32, name="gates", offset=8 * SLAB_BYTES, align_bytes=64)
         turned = pick_pair(1)
         late_grouped = keep.tile([P, 1, 2 * I], BF16, name="late_grouped", align_bytes=64)
         value_grouped = keep.tile([P, 2 * I], BF16, name="value_grouped", align_bytes=64)
         regroup(turned[:], late_grouped[:, 0, :])
-        codes = slabs.tile([P, 2 * Q], U32, name="first_codes", offset=3 * SLAB_BYTES, align_bytes=64)
+        codes = slabs.tile([P, 2 * Q], U32, name="first_codes", offset=2 * SLAB_BYTES, align_bytes=64)
         codes, scales = quantise(first_grouped[:].rearrange("p n c -> p (n c)"), codes[:])
         w_codes, w_scales = codes[:, 0:Q], scales[:, 0:Q]
         sigmoid(gates[:], pair_sums((codes[:, Q:], scales[:, Q:]), "gate_sum")[:])

@@ -23,6 +23,7 @@ PACK = 4
 HALVES = Q // P
 SLAB_BYTES = 4 * T
 SPLIT = 256
+KIB = 1024
 
 
 def tile_attend_gatedvalues_pl_kernel(tc, query, keys_words, keys_scales, size, vals, gval, offs, out_0, out_1, out_2):
@@ -30,23 +31,22 @@ def tile_attend_gatedvalues_pl_kernel(tc, query, keys_words, keys_scales, size, 
     with ExitStack() as ctx:
         keep = ctx.enter_context(tc.tile_pool(name="keep", bufs=1))
         ring = ctx.enter_context(tc.tile_pool(name="ring", bufs=2))
-        slabs = ctx.enter_context(tc.tile_pool(name="slabs", bufs=1))
+        arena = ctx.enter_context(tc.tile_pool(name="arena", bufs=1))
         psum = ctx.enter_context(tc.psum_pool(name="psum", bufs=2))
 
-        key_pool = keep.tile([P, T], U16, name="key_pool", align_bytes=64)
+        def placed(name, shape, dtype, slab, kib=0):
+            return arena.tile(shape, dtype, name=name, offset=slab * SLAB_BYTES + kib * KIB, align_bytes=64)
+
         offsets = keep.tile([P, I // 16], U16, name="offsets")
-        nc.sync.dma_start(key_pool[:].bitcast(I32), keys_words[0].bitcast(I32))
         nc.sync.dma_start(offsets[:], offs)
-        key_scale_pool = keep.tile([P, T], U8, name="key_scale_pool", align_bytes=64)
-        nc.gpsimd.memset(key_scale_pool[:].bitcast(I32), 0)
-        for quad in range(4):
-            nc.sync.dma_start(
-                key_scale_pool[32 * quad : 32 * quad + 4, :].bitcast(I32),
-                keys_scales[0, 4 * quad : 4 * quad + 4, :].bitcast(I32),
-            )
+        key_pool = placed("key_pool", [P, T], U16, 2)
+        nc.sync.dma_start(key_pool[:].bitcast(I32), keys_words[0].bitcast(I32))
+        scale_pool = placed("scale_pool", [P, T], U8, 8)
+        nc.vector.memset(scale_pool[:].bitcast(I32), 0)
+        nc.sync.dma_start(scale_pool[0:P:8, :].bitcast(I32), keys_scales[0].bitcast(I32))
         size_cols = keep.tile([P, PACK], F32, name="size_cols")
         nc.scalar.dma_start(size_cols[:], size.rearrange("o (s r) -> (o s) r", r=PACK))
-        q_raw = keep.tile([P, PACK, Q], F32, name="q_raw")
+        q_raw = placed("q_raw", [P, PACK, Q], F32, 4)
         nc.sync.dma_start(q_raw[:], query.rearrange("(p j) q -> p j q", j=PACK))
 
         gate_rows = gval.rearrange("(p t) c -> p (t c)", t=PACK)
@@ -55,7 +55,7 @@ def tile_attend_gatedvalues_pl_kernel(tc, query, keys_words, keys_scales, size, 
 
         def load(rows, first, count):
             at = len(windows)
-            pool = slabs.tile([P, count * T], F32, name="pool%d" % at, offset=at * SLAB_BYTES, align_bytes=64)
+            pool = placed("pool%d" % at, [P, count * T], F32, at)
             nc.sync.dma_start(pool[:], rows[:, first * T : (first + count) * T])
             windows.extend(pool[:, n * T :] for n in range(count))
 
@@ -63,22 +63,24 @@ def tile_attend_gatedvalues_pl_kernel(tc, query, keys_words, keys_scales, size, 
         ident = keep.tile([P, P], F32, name="ident")
         make_identity(nc, ident[:])
 
-        key_words = keep.tile([P, I], U16, name="key_words", align_bytes=64)
+        picked_scales = placed("picked_scales", [P, I], U8, 6)
+        nc.vector.tensor_copy(picked_scales[:], scale_pool[:].indirect(offsets[:]))
         key_scales = keep.tile([P, I], U8, name="key_scales", align_bytes=64)
+        nc.vector.tensor_copy(key_scales[:].bitcast(I32), picked_scales[:].bitcast(I32))
+        for r in range(1, 4):
+            nc.sync.dma_start(key_scales[r:P:32, :].bitcast(I32), picked_scales[8 * r : P : 32, :].bitcast(I32))
+        key_words = placed("key_words", [P, I], U16, 8)
         nc.vector.tensor_copy(key_words[:], key_pool[:].indirect(offsets[:]))
-        nc.vector.tensor_copy(key_scales[:], key_scale_pool[:].indirect(offsets[:]))
+        load(gate_rows, 2, 2)
 
-        q_bf = keep.tile([P, Q, PACK], BF16, name="q_bf", align_bytes=64)
+        q_bf = placed("q_bf", [P, Q, PACK], BF16, 5)
         nc.scalar.copy(
             q_bf[:].rearrange("p (c i) j -> p c j i", i=4),
             q_raw[:].rearrange("p j (c i) -> p c j i", i=4),
         )
-        q_codes = keep.tile([P, Q], U32, name="q_codes", align_bytes=64)
+        q_codes = placed("q_codes", [P, Q], U32, 7)
         q_scales = keep.tile([P, Q], U8, name="q_scales", align_bytes=64)
         nc.vector.quantize_mx(q_codes[:].bitcast(FP8X4), q_scales[:], q_bf[:].rearrange("p q j -> p (q j)"))
-        load(gate_rows, 2, 2)
-        for t in range(PACK):
-            load(value_rows, t, 1)
 
         size_spread = psum.tile([P, I], F32, name="value_sum")
         for j in range(PACK):
@@ -92,55 +94,6 @@ def tile_attend_gatedvalues_pl_kernel(tc, query, keys_words, keys_scales, size, 
             ACT.Copy, scale=0.5,
         )
 
-        def turn(rows_bf, turned):
-            words = rows_bf.bitcast(F32)
-            for u in range(2):
-                nc.tensor.transpose(turned[:, u, :], words[:, u : 2 * P : 2], ident[:])
-
-        def pick_and_turn(n, turned):
-            if n == 0:
-                picked = slabs.tile([P, I], BF16, name="picked0", offset=9 * SLAB_BYTES, align_bytes=64)
-            elif n == 3:
-                picked = slabs.tile([P, I], BF16, name="picked3", offset=8 * SLAB_BYTES, align_bytes=64)
-            else:
-                picked = ring.tile([P, I], BF16, name="picked", bufs=4, align_bytes=64)
-            if n in (0, 2):
-                nc.scalar.activation(picked[:], windows[n].indirect(offsets[:]), ACT.Copy)
-            elif n in (1, 3):
-                nc.vector.tensor_copy(
-                    picked[:].rearrange("p (u s c) -> p s u c", u=2, c=2), windows[n].indirect(offsets[:])
-                )
-                for u in range(2):
-                    nc.tensor.transpose(turned[:, u, :], picked[:].bitcast(F32)[:, u * P : (u + 1) * P], ident[:])
-                return
-            elif n == 4:
-                nc.vector.tensor_copy(picked[:], windows[n].indirect(offsets[:]))
-            else:
-                nc.vector.tensor_copy(picked[:, 0:SPLIT], windows[n].indirect(offsets[:, 0 : SPLIT // 16]))
-                nc.scalar.activation(
-                    picked[:, SPLIT:I], windows[n].indirect(offsets[:, SPLIT // 16 : I // 16]), ACT.Copy
-                )
-            turn(picked[:], turned)
-
-        def regroup(turned, grouped):
-            nc.scalar.copy(
-                grouped.bitcast(F32).rearrange("p (n e u) -> p n e u", e=P, u=2),
-                turned.rearrange("p n u e -> p n e u"),
-            )
-
-        def quantise(grouped, codes):
-            scales = keep.tile([P, codes.shape[1]], U8, name="scales%d" % len(planes), align_bytes=64)
-            planes.append(scales)
-            nc.vector.quantize_mx(codes.bitcast(FP8X4), scales[:], grouped)
-            return codes, scales[:]
-
-        def pick_pair(k):
-            turned = psum.tile([P, 2, 2, P], F32, name="turned")
-            for n in range(2):
-                pick_and_turn(2 * k + n, turned[:, n])
-            return turned
-
-        planes = []
         scores = []
         for h in range(HALVES):
             cols = slice(h * P, (h + 1) * P)
@@ -151,7 +104,55 @@ def tile_attend_gatedvalues_pl_kernel(tc, query, keys_words, keys_scales, size, 
                 rhs=key_words[:].bitcast(FP4X4), rhs_scale=key_scales[:],
                 start=True, stop=True,
             )
-        neg_max = slabs.tile([P, HALVES], F32, name="neg_max", offset=9 * SLAB_BYTES, align_bytes=64)
+        for t in range(PACK):
+            load(value_rows, t, 1)
+
+        def turn(rows_bf, turned):
+            words = rows_bf.bitcast(F32)
+            for u in range(2):
+                nc.tensor.transpose(turned[:, u, :], words[:, u : 2 * P : 2], ident[:])
+
+        def pick_and_turn(n, turned):
+            picked = ring.tile([P, I], BF16, name="picked", bufs=4, align_bytes=64)
+            if n in (0, 2):
+                nc.scalar.activation(picked[:], windows[n].indirect(offsets[:]), ACT.Copy)
+            elif n in (1, 3):
+                nc.vector.tensor_copy(
+                    picked[:].rearrange("p (u s c) -> p s u c", u=2, c=2), windows[n].indirect(offsets[:])
+                )
+                for u in range(2):
+                    nc.tensor.transpose(turned[:, u, :], picked[:].bitcast(F32)[:, u * P : (u + 1) * P], ident[:])
+                return
+            elif n in (4, 5):
+                nc.vector.tensor_copy(picked[:], windows[n].indirect(offsets[:]))
+            else:
+                nc.vector.tensor_copy(picked[:, 0:SPLIT], windows[n].indirect(offsets[:, 0 : SPLIT // 16]))
+                nc.scalar.activation(
+                    picked[:, SPLIT:I], windows[n].indirect(offsets[:, SPLIT // 16 : I // 16]), ACT.Copy
+                )
+            turn(picked[:], turned)
+
+        def pick(first, count, bank="turned"):
+            turned = psum.tile([P, count, 2, P], F32, name=bank)
+            for n in range(count):
+                pick_and_turn(first + n, turned[:, n])
+            return turned
+
+        def regroup(turned, grouped):
+            nc.scalar.copy(
+                grouped.bitcast(F32).rearrange("p (n e u) -> p n e u", e=P, u=2),
+                turned.rearrange("p n u e -> p n e u"),
+            )
+
+        planes = []
+
+        def quantise(grouped, codes):
+            scales = keep.tile([P, codes.shape[1]], U8, name="scales%d" % len(planes), align_bytes=64)
+            planes.append(scales)
+            nc.vector.quantize_mx(codes.bitcast(FP8X4), scales[:], grouped)
+            return codes, scales[:]
+
+        neg_max = placed("neg_max", [P, HALVES], F32, 9)
         row_sum = keep.tile([P, HALVES], F32, name="row_sum")
         inv_sum = keep.tile([P, HALVES], F32, name="inv_sum")
         prob = keep.tile([P, HALVES, I], F32, name="prob")
@@ -161,18 +162,26 @@ def tile_attend_gatedvalues_pl_kernel(tc, query, keys_words, keys_scales, size, 
                 prob[:, h, :], scores[h][:], ACT.Exp,
                 bias=neg_max[:, h : h + 1], accum_out=row_sum[:, h : h + 1],
             )
-        first_turned = pick_pair(0)
-        nc.vector.reciprocal(inv_sum[:], row_sum[:])
+        first_turned = pick(0, 2, "softmax_bank")
+        first_grouped = placed("first_grouped", [P, 2 * I], BF16, 9)
+        regroup(first_turned[:], first_grouped[:])
         w_turned = psum.tile([P, 2, 2, P], F32, name="softmax_bank")
         for h in range(HALVES):
             w_rows = keep.tile([P, I], BF16, name="w_rows%d" % h, align_bytes=64)
+            nc.vector.reciprocal(inv_sum[:, h : h + 1], row_sum[:, h : h + 1])
             nc.vector.scalar_tensor_tensor(
                 w_rows[:], prob[:, h, :], inv_sum[:, h : h + 1], slot_size[:], ALU.mult, ALU.mult
             )
             turn(w_rows[:], w_turned[:, h])
-        first_grouped = keep.tile([P, 2, 2 * I], BF16, name="first_grouped", align_bytes=64)
-        regroup(first_turned[:], first_grouped[:, 1, :])
-        regroup(w_turned[:], first_grouped[:, 0, :])
+        late_turned = pick(2, 2)
+        w_grouped = placed("w_grouped", [P, 2 * I], BF16, 2)
+        regroup(w_turned[:], w_grouped[:])
+        first_gates = quantise(first_grouped[:], placed("first_codes", [P, 2 * P], U32, 2, 2)[:])
+
+        late_grouped = keep.tile([P, 2 * I], BF16, name="late_grouped", align_bytes=64)
+        regroup(late_turned[:], late_grouped[:])
+        turned4 = pick(4, 1)
+        w_codes, w_scales = quantise(w_grouped[:], placed("w_codes", [P, Q], U32, 4)[:])
 
         def weighted_sum(acc, operand, n, rows=slice(0, Q)):
             codes, scales = operand
@@ -190,44 +199,36 @@ def tile_attend_gatedvalues_pl_kernel(tc, query, keys_words, keys_scales, size, 
                 weighted_sum(sums[:, n, :], operand, n)
             return sums
 
-        def sigmoid(gate, gate_sum):
-            nc.scalar.activation(gate, gate_sum, ACT.Tanh)
-
         def gated(y, half_sum, gate):
             nc.vector.scalar_tensor_tensor(y, gate, 1.0, half_sum, ALU.add, ALU.mult)
 
-        y_rows = out_0.rearrange("(p t) q -> p t q", t=PACK)
-        gates = slabs.tile([P, 2, Q], F32, name="gates", offset=8 * SLAB_BYTES, align_bytes=64)
-        turned = pick_pair(1)
-        late_grouped = keep.tile([P, 1, 2 * I], BF16, name="late_grouped", align_bytes=64)
-        value_grouped = keep.tile([P, 2 * I], BF16, name="value_grouped", align_bytes=64)
-        regroup(turned[:], late_grouped[:, 0, :])
-        codes = slabs.tile([P, 2 * Q], U32, name="first_codes", offset=2 * SLAB_BYTES, align_bytes=64)
-        codes, scales = quantise(first_grouped[:].rearrange("p n c -> p (n c)"), codes[:])
-        w_codes, w_scales = codes[:, 0:Q], scales[:, 0:Q]
-        sigmoid(gates[:], pair_sums((codes[:, Q:], scales[:, Q:]), "gate_sum")[:])
-        for n in range(2):
-            turned = psum.tile([P, 1, 2, P], F32, name="turned")
-            pick_and_turn(4 + n, turned[:, 0])
-            regroup(turned[:], value_grouped[:, n * I : (n + 1) * I])
-            if n == 0:
-                codes = slabs.tile([P, 2 * P], U32, name="gate_codes", offset=4 * SLAB_BYTES, align_bytes=64)
-                late_gate_sums = pair_sums(quantise(late_grouped[:, 0, :], codes[:]), "gate_sum")
-        late_gates = slabs.tile([P, 2, Q], F32, name="late_gates", offset=5 * SLAB_BYTES, align_bytes=64)
-        sigmoid(late_gates[:], late_gate_sums[:])
-        turned = psum.tile([P, 1, 2, P], F32, name="turned")
-        pick_and_turn(6, turned[:, 0])
-        codes = slabs.tile([P, 2 * P], U32, name="late_codes", offset=6 * SLAB_BYTES, align_bytes=64)
-        first_sums = pair_sums(quantise(value_grouped[:], codes[:]), "value_sum")
-
+        first_gate_sums = pair_sums(first_gates, "gate_sum")
+        late_gate_sums = pair_sums(
+            quantise(late_grouped[:], placed("late_codes", [P, 2 * P], U32, 4, 1)[:]), "gate_sum"
+        )
         grouped = ring.tile([P, I], BF16, name="grouped", align_bytes=64)
-        regroup(turned[:, 0:1], grouped[:])
-        turned = psum.tile([P, 1, 2, P], F32, name="turned")
-        pick_and_turn(7, turned[:, 0])
-        codes = slabs.tile([P, P], U32, name="codes6", offset=7 * SLAB_BYTES, align_bytes=64)
+        regroup(turned4[:], grouped[:])
+        gates = keep.tile([P, 2, Q], F32, name="gates")
+        nc.scalar.activation(gates[:], first_gate_sums[:], ACT.Tanh)
+        late_gates = keep.tile([P, 2, Q], F32, name="late_gates")
+        nc.scalar.activation(late_gates[:], late_gate_sums[:], ACT.Tanh)
+
+        first_sums = psum.tile([P, 2, Q], F32, name="value_sum")
+        turned5 = pick(5, 1)
+        weighted_sum(first_sums[:, 0, :], quantise(grouped[:], placed("codes4", [P, P], U32, 5)[:]), 0)
+
+        turned = pick(6, 1)
+        grouped = placed("grouped5", [P, I], BF16, 6)
+        regroup(turned5[:], grouped[:])
+        weighted_sum(first_sums[:, 1, :], quantise(grouped[:], placed("codes5", [P, P], U32, 6, 1)[:]), 0)
+        grouped = ring.tile([P, I], BF16, name="grouped", align_bytes=64)
+        regroup(turned[:], grouped[:])
+
+        turned = pick(7, 1)
         value_sum = psum.tile([P, Q], F32, name="value_sum")
-        weighted_sum(value_sum[:], quantise(grouped[:], codes[:]), 0)
-        y = slabs.tile([P, PACK, Q], F32, name="y", offset=7 * SLAB_BYTES + 2048, align_bytes=64)
+        weighted_sum(value_sum[:], quantise(grouped[:], placed("codes6", [P, P], U32, 7)[:]), 0)
+        y_rows = out_0.rearrange("(p t) q -> p t q", t=PACK)
+        y = placed("y", [P, PACK, Q], F32, 7, 2)
         gated(y[:, 0:2, :], first_sums[:], gates[:])
         nc.sync.dma_start(y_rows[:, 0:2, :], y[:, 0:2, :])
         grouped = y[:, 2, :].bitcast(BF16)

@@ -39,14 +39,14 @@ def tile_attend_gatedvalues_pl_kernel(tc, query, keys_words, keys_scales, size, 
 
         offsets = keep.tile([P, I // 16], U16, name="offsets")
         nc.sync.dma_start(offsets[:], offs)
-        key_pool = placed("key_pool", [P, T], U16, 2)
+        key_pool = placed("key_pool", [P, T], U16, 4)
         nc.sync.dma_start(key_pool[:].bitcast(I32), keys_words[0].bitcast(I32))
         scale_pool = placed("scale_pool", [P, T], U8, 8)
         nc.vector.memset(scale_pool[:].bitcast(I32), 0)
         nc.sync.dma_start(scale_pool[0:P:8, :].bitcast(I32), keys_scales[0].bitcast(I32))
         size_cols = keep.tile([P, PACK], F32, name="size_cols")
         nc.scalar.dma_start(size_cols[:], size.rearrange("o (s r) -> (o s) r", r=PACK))
-        q_raw = placed("q_raw", [P, PACK, Q], F32, 4)
+        q_raw = keep.tile([P, PACK, Q], F32, name="q_raw")
         nc.sync.dma_start(q_raw[:], query.rearrange("(p j) q -> p j q", j=PACK))
 
         gate_rows = gval.rearrange("(p t) c -> p (t c)", t=PACK)
@@ -63,23 +63,23 @@ def tile_attend_gatedvalues_pl_kernel(tc, query, keys_words, keys_scales, size, 
         ident = keep.tile([P, P], F32, name="ident")
         make_identity(nc, ident[:])
 
-        picked_scales = placed("picked_scales", [P, I], U8, 6)
+        picked_scales = placed("picked_scales", [P, I], U8, 2)
         nc.vector.tensor_copy(picked_scales[:], scale_pool[:].indirect(offsets[:]))
         key_scales = keep.tile([P, I], U8, name="key_scales", align_bytes=64)
         nc.vector.tensor_copy(key_scales[:].bitcast(I32), picked_scales[:].bitcast(I32))
         for r in range(1, 4):
-            nc.sync.dma_start(key_scales[r:P:32, :].bitcast(I32), picked_scales[8 * r : P : 32, :].bitcast(I32))
+            nc.sync.dma_start(key_scales[r:P:32, :].bitcast(I32), key_scales[8 * r : P : 32, :].bitcast(I32))
+        load(gate_rows, 2, 2)
         key_words = placed("key_words", [P, I], U16, 8)
         nc.vector.tensor_copy(key_words[:], key_pool[:].indirect(offsets[:]))
-        load(gate_rows, 2, 2)
 
         q_bf = placed("q_bf", [P, Q, PACK], BF16, 5)
         nc.scalar.copy(
             q_bf[:].rearrange("p (c i) j -> p c j i", i=4),
             q_raw[:].rearrange("p j (c i) -> p c j i", i=4),
         )
-        q_codes = placed("q_codes", [P, Q], U32, 7)
-        q_scales = keep.tile([P, Q], U8, name="q_scales", align_bytes=64)
+        q_codes = placed("q_codes", [P, Q], U32, 6)
+        q_scales = placed("q_scales", [P, Q], U8, 7)
         nc.vector.quantize_mx(q_codes[:].bitcast(FP8X4), q_scales[:], q_bf[:].rearrange("p q j -> p (q j)"))
 
         size_spread = psum.tile([P, I], F32, name="value_sum")

@@ -38,9 +38,9 @@ def tile_attend_gatedvalues_pl_kernel(tc, query, keys_words, keys_scales, size, 
             return arena.tile(shape, dtype, name=name, offset=slab * SLAB_BYTES + kib * KIB, align_bytes=64)
 
         offsets = keep.tile([P, I // 16], U16, name="offsets")
-        nc.sync.dma_start(offsets[:], offs)
         key_pool = placed("key_pool", [P, T], U16, 4)
         nc.sync.dma_start(key_pool[:].bitcast(I32), keys_words[0].bitcast(I32))
+        nc.sync.dma_start(offsets[:], offs)
         scale_pool = placed("scale_pool", [P, T], U8, 8)
         nc.vector.memset(scale_pool[:].bitcast(I32), 0)
         nc.sync.dma_start(scale_pool[0:P:8, :].bitcast(I32), keys_scales[0].bitcast(I32))
@@ -113,7 +113,10 @@ def tile_attend_gatedvalues_pl_kernel(tc, query, keys_words, keys_scales, size, 
                 nc.tensor.transpose(turned[:, u, :], words[:, u : 2 * P : 2], ident[:])
 
         def pick_and_turn(n, turned):
-            picked = ring.tile([P, I], BF16, name="picked", bufs=4, align_bytes=64)
+            if n == 7:
+                picked = placed("picked7", [P, I], BF16, 10)
+            else:
+                picked = ring.tile([P, I], BF16, name="picked", bufs=4, align_bytes=64)
             if n in (0, 2):
                 nc.scalar.activation(picked[:], windows[n].indirect(offsets[:]), ACT.Copy)
             elif n in (1, 3):
@@ -123,8 +126,6 @@ def tile_attend_gatedvalues_pl_kernel(tc, query, keys_words, keys_scales, size, 
                 for u in range(2):
                     nc.tensor.transpose(turned[:, u, :], picked[:].bitcast(F32)[:, u * P : (u + 1) * P], ident[:])
                 return
-            elif n in (4, 5):
-                nc.vector.tensor_copy(picked[:], windows[n].indirect(offsets[:]))
             else:
                 nc.vector.tensor_copy(picked[:, 0:SPLIT], windows[n].indirect(offsets[:, 0 : SPLIT // 16]))
                 nc.scalar.activation(
@@ -178,10 +179,10 @@ def tile_attend_gatedvalues_pl_kernel(tc, query, keys_words, keys_scales, size, 
         regroup(w_turned[:], w_grouped[:])
         first_gates = quantise(first_grouped[:], placed("first_codes", [P, 2 * P], U32, 2, 2)[:])
 
-        late_grouped = keep.tile([P, 2 * I], BF16, name="late_grouped", align_bytes=64)
-        regroup(late_turned[:], late_grouped[:])
         turned4 = pick(4, 1)
         w_codes, w_scales = quantise(w_grouped[:], placed("w_codes", [P, Q], U32, 4)[:])
+        late_grouped = placed("late_grouped", [P, 2 * I], BF16, 4, 2)
+        regroup(late_turned[:], late_grouped[:])
 
         def weighted_sum(acc, operand, n, rows=slice(0, Q)):
             codes, scales = operand
@@ -203,28 +204,27 @@ def tile_attend_gatedvalues_pl_kernel(tc, query, keys_words, keys_scales, size, 
             nc.vector.scalar_tensor_tensor(y, gate, 1.0, half_sum, ALU.add, ALU.mult)
 
         first_gate_sums = pair_sums(first_gates, "gate_sum")
-        late_gate_sums = pair_sums(
-            quantise(late_grouped[:], placed("late_codes", [P, 2 * P], U32, 4, 1)[:]), "gate_sum"
-        )
-        grouped = ring.tile([P, I], BF16, name="grouped", align_bytes=64)
-        regroup(turned4[:], grouped[:])
-        gates = keep.tile([P, 2, Q], F32, name="gates")
-        nc.scalar.activation(gates[:], first_gate_sums[:], ACT.Tanh)
-        late_gates = keep.tile([P, 2, Q], F32, name="late_gates")
-        nc.scalar.activation(late_gates[:], late_gate_sums[:], ACT.Tanh)
+        value_grouped = keep.tile([P, 2 * I], BF16, name="value_grouped", align_bytes=64)
+        regroup(turned4[:], value_grouped[:, 0:I])
 
-        first_sums = psum.tile([P, 2, Q], F32, name="value_sum")
-        turned5 = pick(5, 1)
-        weighted_sum(first_sums[:, 0, :], quantise(grouped[:], placed("codes4", [P, P], U32, 5)[:]), 0)
+        turned = pick(5, 1)
+        gates = placed("gates", [P, 2, Q], F32, 5)
+        nc.scalar.activation(gates[:], first_gate_sums[:], ACT.Tanh)
+        regroup(turned[:], value_grouped[:, I : 2 * I])
 
         turned = pick(6, 1)
-        grouped = placed("grouped5", [P, I], BF16, 6)
-        regroup(turned5[:], grouped[:])
-        weighted_sum(first_sums[:, 1, :], quantise(grouped[:], placed("codes5", [P, P], U32, 6, 1)[:]), 0)
+        late_gate_sums = pair_sums(
+            quantise(late_grouped[:], placed("late_codes", [P, 2 * P], U32, 6, 1)[:]), "gate_sum"
+        )
+        first_sums = pair_sums(
+            quantise(value_grouped[:], placed("value_codes", [P, 2 * P], U32, 6)[:]), "value_sum"
+        )
         grouped = ring.tile([P, I], BF16, name="grouped", align_bytes=64)
         regroup(turned[:], grouped[:])
 
         turned = pick(7, 1)
+        gate2 = placed("gate2", [P, Q], F32, 7, 1)
+        nc.scalar.activation(gate2[:], late_gate_sums[:, 0, :], ACT.Tanh)
         value_sum = psum.tile([P, Q], F32, name="value_sum")
         weighted_sum(value_sum[:], quantise(grouped[:], placed("codes6", [P, P], U32, 7)[:]), 0)
         y_rows = out_0.rearrange("(p t) q -> p t q", t=PACK)
@@ -233,16 +233,18 @@ def tile_attend_gatedvalues_pl_kernel(tc, query, keys_words, keys_scales, size, 
         nc.sync.dma_start(y_rows[:, 0:2, :], y[:, 0:2, :])
         grouped = y[:, 2, :].bitcast(BF16)
         regroup(turned[:], grouped)
+        gate3 = placed("gate3", [P, Q], F32, 10)
+        nc.scalar.activation(gate3[:], late_gate_sums[:, 1, :], ACT.Tanh)
         y_bf = keep.tile([P, Q, PACK], BF16, name="y_bf", align_bytes=64)
         codes = keep.tile([P, P], U32, name="codes7", align_bytes=64)
         operand = quantise(grouped, codes[:])
         halves = [slice(h * P, (h + 1) * P) for h in range(HALVES)]
-        last_sums = [psum.tile([P, P], F32, name="gate_sum") for h in range(HALVES)]
+        last_sums = [psum.tile([P, P], F32, name="softmax_bank") for h in range(HALVES)]
         for h in range(HALVES):
             weighted_sum(last_sums[h][:], operand, 0, halves[h])
-        gated(y[:, 2, :], value_sum[:], late_gates[:, 0, :])
+        gated(y[:, 2, :], value_sum[:], gate2[:])
         for h in range(HALVES):
-            gated(y[:, 3, halves[h]], last_sums[h][:], late_gates[:, 1, halves[h]])
+            gated(y[:, 3, halves[h]], last_sums[h][:], gate3[:, halves[h]])
         nc.sync.dma_start(y_rows[:, 2:4, :], y[:, 2:4, :])
         for copy, rows in (
             (nc.scalar.copy, slice(0, P // 2)),

from contextlib import ExitStack

import concourse.mybir as mybir
from concourse.masks import make_identity

D, T, I, Q, E = 512, 2048, 512, 256, 512
FLOPS = 2 * Q * I * (D + 2 * E)

F32 = mybir.dt.float32
BF16 = mybir.dt.bfloat16
I32 = mybir.dt.int32
U32 = mybir.dt.uint32
U16 = mybir.dt.uint16
U8 = mybir.dt.uint8
FP8X4 = mybir.dt.float8_e4m3fn_x4
FP4X4 = mybir.dt.float4_e2m1fn_x4
ACT = mybir.ActivationFunctionType
ALU = mybir.AluOpType
AXIS = mybir.AxisListType

P = 128
PACK = 4
HALVES = Q // P
SLAB_BYTES = 4 * T
SPLIT = 256
KIB = 1024


def tile_attend_gatedvalues_pl_kernel(tc, query, keys_words, keys_scales, size, vals, gval, offs, out_0, out_1, out_2):
    nc = tc.nc
    with ExitStack() as ctx:
        keep = ctx.enter_context(tc.tile_pool(name="keep", bufs=1))
        ring = ctx.enter_context(tc.tile_pool(name="ring", bufs=2))
        arena = ctx.enter_context(tc.tile_pool(name="arena", bufs=1))
        psum = ctx.enter_context(tc.psum_pool(name="psum", bufs=2))

        def placed(name, shape, dtype, slab, kib=0):
            return arena.tile(shape, dtype, name=name, offset=slab * SLAB_BYTES + kib * KIB, align_bytes=64)

        offsets = keep.tile([P, I // 16], U16, name="offsets")
        key_pool = placed("key_pool", [P, T], U16, 4)
        nc.sync.dma_start(key_pool[:].bitcast(I32), keys_words[0].bitcast(I32))
        nc.sync.dma_start(offsets[:], offs)
        scale_pool = placed("scale_pool", [P, T], U8, 8)
        nc.vector.memset(scale_pool[:].bitcast(I32), 0)
        nc.sync.dma_start(scale_pool[0:P:8, :].bitcast(I32), keys_scales[0].bitcast(I32))
        size_cols = keep.tile([P, PACK], F32, name="size_cols")
        nc.scalar.dma_start(size_cols[:], size.rearrange("o (s r) -> (o s) r", r=PACK))
        q_raw = keep.tile([P, PACK, Q], F32, name="q_raw")
        nc.sync.dma_start(q_raw[:], query.rearrange("(p j) q -> p j q", j=PACK))

        gate_rows = gval.rearrange("(p t) c -> p (t c)", t=PACK)
        value_rows = vals.rearrange("(p t) c -> p (t c)", t=PACK)
        windows = []

        def load(rows, first, count):
            at = len(windows)
            pool = placed("pool%d" % at, [P, count * T], F32, at)
            nc.sync.dma_start(pool[:], rows[:, first * T : (first + count) * T])
            windows.extend(pool[:, n * T :] for n in range(count))

        load(gate_rows, 0, 2)
        ident = keep.tile([P, P], F32, name="ident")
        make_identity(nc, ident[:])

        picked_scales = placed("picked_scales", [P, I], U8, 2)
        nc.vector.tensor_copy(picked_scales[:], scale_pool[:].indirect(offsets[:]))
        key_scales = keep.tile([P, I], U8, name="key_scales", align_bytes=64)
        nc.vector.tensor_copy(key_scales[:].bitcast(I32), picked_scales[:].bitcast(I32))
        for r in range(1, 4):
            nc.sync.dma_start(key_scales[r:P:32, :].bitcast(I32), key_scales[8 * r : P : 32, :].bitcast(I32))
        load(gate_rows, 2, 2)
        key_words = placed("key_words", [P, I], U16, 8)
        nc.vector.tensor_copy(key_words[:], key_pool[:].indirect(offsets[:]))

        q_bf = placed("q_bf", [P, Q, PACK], BF16, 5)
        nc.scalar.copy(
            q_bf[:].rearrange("p (c i) j -> p c j i", i=4),
            q_raw[:].rearrange("p j (c i) -> p c j i", i=4),
        )
        q_codes = placed("q_codes", [P, Q], U32, 6)
        q_scales = placed("q_scales", [P, Q], U8, 7)
        nc.vector.quantize_mx(q_codes[:].bitcast(FP8X4), q_scales[:], q_bf[:].rearrange("p q j -> p (q j)"))

        size_spread = psum.tile([P, I], F32, name="value_sum")
        for j in range(PACK):
            nc.tensor.transpose(
                size_spread[:, j * P : (j + 1) * P], size_cols[:, j : j + 1].to_broadcast([P, P]), ident[:]
            )
        slot_size = keep.tile([P, I], F32, name="slot_size")
        nc.scalar.activation(
            slot_size[:].rearrange("p (s r) -> p s r", r=PACK),
            size_spread[:].rearrange("p (r s) -> p s r", r=PACK),
            ACT.Copy, scale=0.5,
        )

        scores = []
        for h in range(HALVES):
            cols = slice(h * P, (h + 1) * P)
            scores.append(psum.tile([P, I], F32, name="softmax_bank"))
            nc.tensor.matmul_mx(
                scores[h][:],
                lhsT=q_codes[:, cols].bitcast(FP8X4), lhsT_scale=q_scales[:, cols],
                rhs=key_words[:].bitcast(FP4X4), rhs_scale=key_scales[:],
                start=True, stop=True,
            )
        for t in range(PACK):
            load(value_rows, t, 1)

        def turn(rows_bf, turned):
            words = rows_bf.bitcast(F32)
            for u in range(2):
                nc.tensor.transpose(turned[:, u, :], words[:, u : 2 * P : 2], ident[:])

        def pick_and_turn(n, turned):
            if n == 7:
                picked = placed("picked7", [P, I], BF16, 10)
            else:
                picked = ring.tile([P, I], BF16, name="picked", bufs=4, align_bytes=64)
            if n in (0, 2):
                nc.scalar.activation(picked[:], windows[n].indirect(offsets[:]), ACT.Copy)
            elif n in (1, 3):
                nc.vector.tensor_copy(
                    picked[:].rearrange("p (u s c) -> p s u c", u=2, c=2), windows[n].indirect(offsets[:])
                )
                for u in range(2):
                    nc.tensor.transpose(turned[:, u, :], picked[:].bitcast(F32)[:, u * P : (u + 1) * P], ident[:])
                return
            else:
                nc.vector.tensor_copy(picked[:, 0:SPLIT], windows[n].indirect(offsets[:, 0 : SPLIT // 16]))
                nc.scalar.activation(
                    picked[:, SPLIT:I], windows[n].indirect(offsets[:, SPLIT // 16 : I // 16]), ACT.Copy
                )
            turn(picked[:], turned)

        def pick(first, count, bank="turned"):
            turned = psum.tile([P, count, 2, P], F32, name=bank)
            for n in range(count):
                pick_and_turn(first + n, turned[:, n])
            return turned

        def regroup(turned, grouped):
            nc.scalar.copy(
                grouped.bitcast(F32).rearrange("p (n e u) -> p n e u", e=P, u=2),
                turned.rearrange("p n u e -> p n e u"),
            )

        planes = []

        def quantise(grouped, codes):
            scales = keep.tile([P, codes.shape[1]], U8, name="scales%d" % len(planes), align_bytes=64)
            planes.append(scales)
            nc.vector.quantize_mx(codes.bitcast(FP8X4), scales[:], grouped)
            return codes, scales[:]

        neg_max = placed("neg_max", [P, HALVES], F32, 9)
        row_sum = keep.tile([P, HALVES], F32, name="row_sum")
        inv_sum = keep.tile([P, HALVES], F32, name="inv_sum")
        prob = keep.tile([P, HALVES, I], F32, name="prob")
        for h in range(HALVES):
            nc.vector.tensor_reduce(neg_max[:, h : h + 1], scores[h][:], AXIS.X, ALU.max, negate=True)
            nc.scalar.activation(
                prob[:, h, :], scores[h][:], ACT.Exp,
                bias=neg_max[:, h : h + 1], accum_out=row_sum[:, h : h + 1],
            )
        first_turned = pick(0, 2, "softmax_bank")
        first_grouped = placed("first_grouped", [P, 2 * I], BF16, 9)
        regroup(first_turned[:], first_grouped[:])
        w_turned = psum.tile([P, 2, 2, P], F32, name="softmax_bank")
        for h in range(HALVES):
            w_rows = keep.tile([P, I], BF16, name="w_rows%d" % h, align_bytes=64)
            nc.vector.reciprocal(inv_sum[:, h : h + 1], row_sum[:, h : h + 1])
            nc.vector.scalar_tensor_tensor(
                w_rows[:], prob[:, h, :], inv_sum[:, h : h + 1], slot_size[:], ALU.mult, ALU.mult
            )
            turn(w_rows[:], w_turned[:, h])
        late_turned = pick(2, 2)
        w_grouped = placed("w_grouped", [P, 2 * I], BF16, 2)
        regroup(w_turned[:], w_grouped[:])
        first_gates = quantise(first_grouped[:], placed("first_codes", [P, 2 * P], U32, 2, 2)[:])

        turned4 = pick(4, 1)
        w_codes, w_scales = quantise(w_grouped[:], placed("w_codes", [P, Q], U32, 4)[:])
        late_grouped = placed("late_grouped", [P, 2 * I], BF16, 4, 2)
        regroup(late_turned[:], late_grouped[:])

        def weighted_sum(acc, operand, n, rows=slice(0, Q)):
            codes, scales = operand
            cols = slice(n * P, (n + 1) * P)
            nc.tensor.matmul_mx(
                acc,
                lhsT=codes[:, cols].bitcast(FP8X4), lhsT_scale=scales[:, cols],
                rhs=w_codes[:, rows].bitcast(FP8X4), rhs_scale=w_scales[:, rows],
                start=True, stop=True,
            )

        def pair_sums(operand, name):
            sums = psum.tile([P, 2, Q], F32, name=name)
            for n in range(2):
                weighted_sum(sums[:, n, :], operand, n)
            return sums

        def gated(y, half_sum, gate):
            nc.vector.scalar_tensor_tensor(y, gate, 1.0, half_sum, ALU.add, ALU.mult)

        first_gate_sums = pair_sums(first_gates, "gate_sum")
        value_grouped = keep.tile([P, 2 * I], BF16, name="value_grouped", align_bytes=64)
        regroup(turned4[:], value_grouped[:, 0:I])

        turned = pick(5, 1)
        gates = placed("gates", [P, 2, Q], F32, 5)
        nc.scalar.activation(gates[:], first_gate_sums[:], ACT.Tanh)
        regroup(turned[:], value_grouped[:, I : 2 * I])

        turned = pick(6, 1)
        late_gate_sums = pair_sums(
            quantise(late_grouped[:], placed("late_codes", [P, 2 * P], U32, 6, 1)[:]), "gate_sum"
        )
        first_sums = pair_sums(
            quantise(value_grouped[:], placed("value_codes", [P, 2 * P], U32, 6)[:]), "value_sum"
        )
        grouped = ring.tile([P, I], BF16, name="grouped", align_bytes=64)
        regroup(turned[:], grouped[:])

        turned = pick(7, 1)
        gate2 = placed("gate2", [P, Q], F32, 7, 1)
        nc.scalar.activation(gate2[:], late_gate_sums[:, 0, :], ACT.Tanh)
        value_sum = psum.tile([P, Q], F32, name="value_sum")
        weighted_sum(value_sum[:], quantise(grouped[:], placed("codes6", [P, P], U32, 7)[:]), 0)
        y_rows = out_0.rearrange("(p t) q -> p t q", t=PACK)
        y = placed("y", [P, PACK, Q], F32, 7, 2)
        gated(y[:, 0:2, :], first_sums[:], gates[:])
        nc.sync.dma_start(y_rows[:, 0:2, :], y[:, 0:2, :])
        grouped = y[:, 2, :].bitcast(BF16)
        regroup(turned[:], grouped)
        gate3 = placed("gate3", [P, Q], F32, 10)
        nc.scalar.activation(gate3[:], late_gate_sums[:, 1, :], ACT.Tanh)
        y_bf = keep.tile([P, Q, PACK], BF16, name="y_bf", align_bytes=64)
        codes = keep.tile([P, P], U32, name="codes7", align_bytes=64)
        operand = quantise(grouped, codes[:])
        halves = [slice(h * P, (h + 1) * P) for h in range(HALVES)]
        last_sums = [psum.tile([P, P], F32, name="softmax_bank") for h in range(HALVES)]
        for h in range(HALVES):
            weighted_sum(last_sums[h][:], operand, 0, halves[h])
        gated(y[:, 2, :], value_sum[:], gate2[:])
        for h in range(HALVES):
            gated(y[:, 3, halves[h]], last_sums[h][:], gate3[:, halves[h]])
        nc.sync.dma_start(y_rows[:, 2:4, :], y[:, 2:4, :])
        for copy, rows in (
            (nc.scalar.copy, slice(0, P // 2)),
            (nc.vector.tensor_copy, slice(P // 2, P)),
            (nc.vector.tensor_copy, halves[1]),
        ):
            copy(
                y_bf[:, rows, :].rearrange("p (c i) t -> p c t i", i=4),
                y[:, :, rows].rearrange("p t (c i) -> p c t i", i=4),
            )

        y_codes = keep.tile([P, Q], U32, name="y_codes", align_bytes=64)
        y_scales = keep.tile([P, Q], U8, name="y_scales", align_bytes=64)
        for h in range(HALVES):
            nc.vector.quantize_mx(
                y_codes[:, halves[h]].bitcast(FP8X4), y_scales[:, halves[h]],
                y_bf[:, halves[h], :].rearrange("p q j -> p (q j)"),
            )
            queue = nc.scalar if h == 0 else nc.sync
            queue.dma_start(
                out_1[0, :, halves[h], :].rearrange("p q j -> p (q j)").bitcast(I32), y_codes[:, halves[h]].bitcast(I32)
            )
        for quad in range(4):
            queue = nc.scalar if quad % 2 == 0 else nc.sync
            queue.dma_start(
                out_2[0, 4 * quad : 4 * quad + 4, :].bitcast(I32),
                y_scales[32 * quad : 32 * quad + 4, :].bitcast(I32),
            )
